import numpy as np
import ml_dtypes


def mxq(x, axis, fmt="e4m3"):
    dtype, down = {"e4m3": (ml_dtypes.float8_e4m3fn, 7), "e5m2": (ml_dtypes.float8_e5m2, 14)}[fmt]
    v = np.moveaxis(np.asarray(x, np.float32).astype(ml_dtypes.bfloat16).astype(np.float64), axis, -1)
    blocks = v.reshape(v.shape[:-1] + (-1, 32))
    amax = np.abs(blocks).max(-1, keepdims=True)
    byte = np.maximum(np.where(amax > 0, np.frexp(amax)[1] - 1 + 127, 0) - down, 1)
    scale = np.exp2(byte - 127.0)
    codes = (blocks / scale).astype(np.float32).astype(dtype).astype(np.float64)
    return np.moveaxis((codes * scale).reshape(v.shape), -1, axis)


WIDE = False


def mx_kscale(k):
    if not WIDE:
        return np.ones(k)
    levels = np.array([10, -10, 5, -5, 0])
    if k % 512:
        return np.exp2(np.random.permutation(np.resize(levels, k // 32))).repeat(32)
    a = np.empty((k // 512, 16))
    for p in range(k // 512):
        a[p, :8] = np.random.permutation(np.resize(levels, 8))
        for g in range(8):
            far = levels[np.abs(levels - a[p, g]) >= 10]
            a[p, g + 8] = far[np.random.randint(len(far))]
    return np.exp2(a.ravel()).repeat(32)


def f64(x):
    return np.asarray(x).astype(np.float64)


def striped(idx):
    return np.tile(np.asarray(idx).reshape(-1, 16).T, (8, 1)).astype(np.uint16)


def unstriped(offs):
    return offs[:16].T.reshape(-1).astype(np.int64)


E2M1 = np.array([0.0, 0.5, 1.0, 1.5, 2.0, 3.0, 4.0, 6.0, -0.0, -0.5, -1.0, -1.5, -2.0, -3.0, -4.0, -6.0])


def pack_weight(w, fmt):
    k, n = w.shape
    w = f64(np.asarray(w, np.float32).astype(ml_dtypes.bfloat16)).reshape(k // 32, 32, n)
    amax = np.abs(w).max(1)
    if fmt == "e4m3":
        byte = np.frexp(amax)[1] - 1 + 127 - 7
    else:
        mant, ex = np.frexp(amax / 6.0)
        byte = np.where(mant > 0.5, ex, ex - 1) + 127
    byte = np.clip(np.where(amax > 0, byte, 1), 1, 254)
    scaled = (w * np.exp2(127.0 - byte)[:, None, :]).reshape(k, n).astype(np.float32)
    by_word = np.ascontiguousarray(scaled.reshape(k // 512, 128, 4, n).transpose(0, 1, 3, 2))
    if fmt == "e4m3":
        words = by_word.astype(ml_dtypes.float8_e4m3fn).view(np.uint8)
    else:
        c = by_word.astype(ml_dtypes.float4_e2m1fn).view(np.uint8) & 0xF
        words = (c[..., 0::2] | (c[..., 1::2] << 4)).reshape(k // 512, 128, 2 * n)
    return np.ascontiguousarray(words), np.ascontiguousarray(byte.astype(np.uint8).reshape(k // 512, 16, n))


def unpack_weight(words, scales, fmt):
    g, _, n = scales.shape
    words = np.ascontiguousarray(words).reshape(g, 128, n, -1)
    if fmt == "e4m3":
        vals = words.view(ml_dtypes.float8_e4m3fn).astype(np.float64)
    else:
        nib = np.empty((g, 128, n, 4), np.uint8)
        nib[..., 0::2] = words & 0xF
        nib[..., 1::2] = words >> 4
        vals = E2M1[nib]
    vals = vals * np.repeat(np.exp2(scales.astype(np.float64) - 127.0), 8, axis=1)[..., None]
    return vals.transpose(0, 1, 3, 2).reshape(g * 512, n)


B, N, T, D, NQ = 1, 512, 2048, 512, 512
DV = 512


def sgn(shape):
    return np.random.uniform(0.5, 2.0, shape) * np.where(np.random.standard_normal(shape) < 0, -1.0, 1.0)


def setup_inputs():
    n = np.random.standard_normal
    idx = np.random.permutation(T)[:B * N]
    s = mx_kscale(D)[:, None]
    u = mx_kscale(N)
    ut = np.ones(T)
    ut[idx] = u
    kp = pack_weight(n((D, T)) / s, "e4m3")
    return {
        "qT": (n((B, D, NQ)) * s * (1.00 / np.sqrt(D))).astype(np.float32),
        "k_words": kp[0],
        "k_scales": kp[1],
        "vT": (n((DV, T)) / ut).astype(np.float32),
        "us": (sgn((B, N, 1)) * u[:, None]).astype(np.float32),
        "offs": striped(idx),
    }


def reference(qT, k_words, k_scales, vT, us, offs):
    idx = unstriped(offs)
    pick = lambda x, which: x[:, which].reshape(x.shape[0], B, -1).transpose(1, 0, 2)
    k = unpack_weight(k_words, k_scales, "e4m3")
    kg = pick(k, idx)
    qq = mxq(f64(qT), 1, "e4m3")
    a = kg.transpose(0, 2, 1) @ qq
    y = np.maximum(a, 0.0) * f64(us)
    wq = mxq(y, 1, "e4m3")
    o = wq.transpose(0, 2, 1) @ mxq(pick(f64(vT), idx).transpose(0, 2, 1), 1, "e4m3")
    return o

@@ -1,0 +1,191 @@
+from contextlib import ExitStack
+
+import concourse.mybir as mybir
+from concourse.masks import make_identity
+
+F32 = mybir.dt.float32
+BF16 = mybir.dt.bfloat16
+I32 = mybir.dt.int32
+U32 = mybir.dt.uint32
+U16 = mybir.dt.uint16
+U8 = mybir.dt.uint8
+FP8X4 = mybir.dt.float8_e4m3fn_x4
+ALU = mybir.AluOpType
+ACT = mybir.ActivationFunctionType
+
+P = 128
+PACK = 4
+SLOTS = 512
+POOL = 2048
+D = 512
+NQ = 512
+DV = 512
+BLOCKS = 4
+
+FLOPS = 2 * SLOTS * NQ * D + 2 * SLOTS * NQ * DV
+
+
+def tile_attend_mlp_relu_topk_kernel(tc, qT, k_words, k_scales, vT, us, offs, out):
+    nc = tc.nc
+    with ExitStack() as ctx:
+        keep = ctx.enter_context(tc.tile_pool(name="keep", bufs=1))
+        psum = ctx.enter_context(tc.psum_pool(name="psum", bufs=1))
+
+        offsets = keep.tile([P, SLOTS // 16], U16, name="offsets")
+        kw = keep.tile([P, POOL], I32, name="kw", align_bytes=64)
+        ks = keep.tile([P, POOL // 4], I32, name="ks", align_bytes=64)
+        q_raw = [keep.tile([P, PACK, NQ // 2], F32, name="q_raw%d" % h, align_bytes=64) for h in range(2)]
+        us_sb = keep.tile([P, 1, PACK], F32, name="us_sb")
+        v_raw = [keep.tile([P, POOL], F32, name="v_raw%d" % c, align_bytes=64) for c in range(BLOCKS)]
+        ident = keep.tile([P, P], F32, name="ident", align_bytes=64)
+
+        nc.vector.memset(ks[:], 0)
+        nc.sync.dma_start(offsets[:], offs)
+        q_rows = qT[0].rearrange("(p j) w -> p j w", j=PACK)
+        nc.sync.dma_start(q_raw[0][:], q_rows[:, :, 0 : 2 * P])
+        for g in range(4):
+            nc.sync.dma_start(ks[32 * g : 32 * g + 4, :], k_scales[0, 4 * g : 4 * g + 4, :].bitcast(I32))
+        nc.sync.dma_start(kw[:], k_words[0].rearrange("p t r -> p (t r)").bitcast(I32))
+        nc.sync.dma_start(q_raw[1][:], q_rows[:, :, 2 * P : NQ])
+        nc.sync.dma_start(us_sb[:], us[0].rearrange("(p t) o -> p o t", t=PACK))
+        for c in range(BLOCKS):
+            nc.sync.dma_start(v_raw[c][:], vT[c * P : (c + 1) * P, :])
+        make_identity(nc, ident[:])
+
+        kg = keep.tile([P, SLOTS], U32, name="kg", align_bytes=64)
+        ksl = keep.tile([P, SLOTS], U8, name="ksl", align_bytes=64)
+        ksg = keep.tile([P, SLOTS], U8, name="ksg", align_bytes=64)
+
+        q_bf = [keep.tile([P, 2 * P * PACK], BF16, name="q_bf%d" % h, align_bytes=64) for h in range(2)]
+        q_c = keep.tile([P, NQ], U32, name="q_c", align_bytes=64)
+        q_s = keep.tile([P, NQ], U8, name="q_s", align_bytes=64)
+        y_bf = [q_bf[1][:, 0 : P * PACK]]
+        y_bf += [keep.tile([P, P * PACK], BF16, name="y_bf%d" % b, align_bytes=64) for b in range(1, BLOCKS)]
+        y_c = [keep.tile([P, P], U32, name="y_c%d" % b, align_bytes=64) for b in range(BLOCKS)]
+        y_s = [keep.tile([P, P], U8, name="y_s%d" % b, align_bytes=64) for b in range(BLOCKS)]
+        a_ps = [psum.tile([P, PACK, P], F32, name="acc", bufs=6) for b in range(BLOCKS)]
+
+        def q_cast(h):
+            nc.scalar.copy(
+                q_bf[h][:].rearrange("p (w j) -> p w j", j=PACK),
+                q_raw[h][:].rearrange("p j w -> p w j"),
+            )
+
+        def q_quant(h):
+            cols = slice(h * 2 * P, (h + 1) * 2 * P)
+            nc.vector.quantize_mx(out=q_c[:, cols].bitcast(FP8X4), scales=q_s[:, cols], in_=q_bf[h][:])
+
+        def first(blocks):
+            for b in blocks:
+                for t in range(PACK):
+                    cols = slice(t * P, (t + 1) * P)
+                    nc.tensor.matmul_mx(
+                        out=a_ps[b][:, t, :],
+                        lhsT=kg[:, cols].bitcast(FP8X4),
+                        lhsT_scale=ksg[:, cols],
+                        rhs=q_c[:, b * P : (b + 1) * P].bitcast(FP8X4),
+                        rhs_scale=q_s[:, b * P : (b + 1) * P],
+                        start=True,
+                        stop=True,
+                    )
+
+        def y_make(b):
+            nc.vector.scalar_tensor_tensor(
+                out=y_bf[b][:].rearrange("p (w t) -> p w t", t=PACK),
+                in0=a_ps[b][:].rearrange("p t w -> p w t"),
+                scalar=0.0,
+                in1=us_sb[:].to_broadcast([P, P, PACK]),
+                op0=ALU.max,
+                op1=ALU.mult,
+            )
+
+        def y_quant(b):
+            nc.vector.quantize_mx(out=y_c[b][:].bitcast(FP8X4), scales=y_s[b][:], in_=y_bf[b][:])
+
+        v_bf01 = keep.tile([P, 2 * P * PACK], BF16, name="v_bf01", align_bytes=64)
+        v_bf = [v_bf01[:, 0 : P * PACK], v_bf01[:, P * PACK : 2 * P * PACK]]
+        v_bf += [keep.tile([P, P * PACK], BF16, name="v_bf%d" % c, align_bytes=64) for c in range(2, BLOCKS)]
+        v_g0 = keep.tile([P, SLOTS], BF16, name="v_g0", align_bytes=64)
+        v_half = keep.tile([P, POOL], BF16, name="v_half", align_bytes=64)
+        v_g = [v_g0, y_bf[2], y_bf[3], v_bf[1]]
+        v_s = keep.tile([P, DV], U8, name="v_s", align_bytes=64)
+
+        def v_gather(c):
+            placed = v_g[c][:].rearrange("p (u m j) -> p m u j", u=2, j=2)
+            if c == 0:
+                nc.scalar.activation(v_half[:], v_raw[c][:], ACT.Copy)
+                nc.scalar.activation(placed, v_half[:].indirect(offsets[:]), ACT.Copy)
+            else:
+                nc.vector.tensor_copy(placed, v_raw[c][:].indirect(offsets[:]))
+            words = v_g[c][:].bitcast(F32)
+            t_ps = psum.tile([P, 2, P], F32, name="t_ps", bufs=2)
+            for u in range(2):
+                nc.tensor.transpose(t_ps[:, u, :], words[:, u * P : (u + 1) * P], ident[:])
+            nc.scalar.copy(
+                v_bf[c][:].bitcast(F32).rearrange("p (e u) -> p e u", u=2),
+                t_ps[:].rearrange("p u e -> p e u"),
+            )
+
+        def v_quant(values, e0, ne, tag):
+            codes = keep.tile([P, ne], U32, name=tag, align_bytes=64)
+            nc.vector.quantize_mx(out=codes[:].bitcast(FP8X4), scales=v_s[:, e0 : e0 + ne], in_=values)
+            return codes
+
+        out_v = out[0].rearrange("(b p) e -> p b e", p=P)
+
+        def second(codes, b0, nb, e0, ne, res, copy):
+            o_ps = psum.tile([P, nb, ne], F32, name="acc", bufs=6)
+            cols = slice(e0, e0 + ne)
+            for b in range(nb):
+                nc.tensor.matmul_mx(
+                    out=o_ps[:, b, :],
+                    lhsT=y_c[b0 + b][:].bitcast(FP8X4),
+                    lhsT_scale=y_s[b0 + b][:],
+                    rhs=codes[:].bitcast(FP8X4),
+                    rhs_scale=v_s[:, cols],
+                    start=True,
+                    stop=True,
+                )
+            copy(res, o_ps[:])
+
+        res01 = [keep.tile([P, 2, 2 * P], F32, name="res01_%d" % h) for h in range(2)]
+        res2 = keep.tile([P, BLOCKS, P], F32, name="res2")
+        res3 = [keep.tile([P, 2, P], F32, name="res3_%d" % h) for h in range(2)]
+
+        q_cast(0)
+        nc.vector.tensor_copy(ksl[:], ks[:].bitcast(U8).indirect(offsets[:]))
+        q_quant(0)
+        nc.vector.tensor_copy(
+            ksg[:].rearrange("p (t m) -> p t m", t=PACK), ksl[:].rearrange("p (m t) -> p t m", t=PACK)
+        )
+        nc.vector.tensor_copy(
+            kg[:].rearrange("p (t m) -> p m t", t=PACK), kw[:].bitcast(U32).indirect(offsets[:])
+        )
+        first((0, 1))
+        q_cast(1)
+        q_quant(1)
+        first((2, 3))
+        y_make(0)
+        y_make(1)
+        y_quant(0)
+        y_make(2)
+        y_quant(1)
+        y_make(3)
+        y_quant(2)
+        v_gather(0)
+        v_gather(1)
+        y_quant(3)
+        v_gather(2)
+        codes01 = v_quant(v_bf01[:], 0, 2 * P, "v_raw2")
+        for h in range(2):
+            second(codes01, 2 * h, 2, 0, 2 * P, res01[h][:], nc.scalar.copy)
+            nc.sync.dma_start(out_v[:, 2 * h : 2 * h + 2, 0 : 2 * P], res01[h][:])
+        v_gather(3)
+        codes2 = v_quant(v_bf[2][:], 2 * P, P, "v_raw3")
+        second(codes2, 0, BLOCKS, 2 * P, P, res2[:], nc.scalar.copy)
+        nc.sync.dma_start(out_v[:, :, 2 * P : 3 * P], res2[:])
+        codes3 = v_quant(v_bf[3][:], 3 * P, P, "codes3")
+        second(codes3, 0, 2, 3 * P, P, res3[0][:], nc.vector.tensor_copy)
+        nc.sync.dma_start(out_v[:, 0:2, 3 * P : DV], res3[0][:])
+        second(codes3, 2, 2, 3 * P, P, res3[1][:], nc.scalar.copy)
+        nc.scalar.dma_start(out_v[:, 2:4, 3 * P : DV], res3[1][:])

@@ -35,6 +35,8 @@ def tile_attend_mlp_relu_topk_kernel(tc, qT, k_words, k_scales, vT, us, offs, ou
         kw = keep.tile([P, POOL], I32, name="kw", align_bytes=64)
         ks = keep.tile([P, POOL // 4], I32, name="ks", align_bytes=64)
         q_raw = [keep.tile([P, PACK, NQ // 2], F32, name="q_raw%d" % h, align_bytes=64) for h in range(2)]
+        us_row = keep.tile([1, SLOTS], F32, name="us_row")
+        us_wide = keep.tile([P, SLOTS], F32, name="us_wide", align_bytes=64)
         us_sb = keep.tile([P, 1, PACK], F32, name="us_sb")
         v_raw = [keep.tile([P, POOL], F32, name="v_raw%d" % c, align_bytes=64) for c in range(BLOCKS)]
         ident = keep.tile([P, P], F32, name="ident", align_bytes=64)
@@ -45,25 +47,26 @@ def tile_attend_mlp_relu_topk_kernel(tc, qT, k_words, k_scales, vT, us, offs, ou
         nc.sync.dma_start(q_raw[0][:], q_rows[:, :, 0 : 2 * P])
         for g in range(4):
             nc.sync.dma_start(ks[32 * g : 32 * g + 4, :], k_scales[0, 4 * g : 4 * g + 4, :].bitcast(I32))
+        nc.sync.dma_start(us_row[:], us[0].rearrange("s o -> o s"))
         nc.sync.dma_start(kw[:], k_words[0].rearrange("p t r -> p (t r)").bitcast(I32))
         nc.sync.dma_start(q_raw[1][:], q_rows[:, :, 2 * P : NQ])
-        nc.sync.dma_start(us_sb[:], us[0].rearrange("(p t) o -> p o t", t=PACK))
         for c in range(BLOCKS):
             nc.sync.dma_start(v_raw[c][:], vT[c * P : (c + 1) * P, :])
         make_identity(nc, ident[:])
+        nc.gpsimd.memset(us_wide[:], 0.0)
 
         kg = keep.tile([P, SLOTS], U32, name="kg", align_bytes=64)
         ksl = keep.tile([P, SLOTS], U8, name="ksl", align_bytes=64)
         ksg = keep.tile([P, SLOTS], U8, name="ksg", align_bytes=64)
 
         q_bf = [keep.tile([P, 2 * P * PACK], BF16, name="q_bf%d" % h, align_bytes=64) for h in range(2)]
-        q_c = keep.tile([P, NQ], U32, name="q_c", align_bytes=64)
-        q_s = keep.tile([P, NQ], U8, name="q_s", align_bytes=64)
-        y_bf = [q_bf[1][:, 0 : P * PACK]]
-        y_bf += [keep.tile([P, P * PACK], BF16, name="y_bf%d" % b, align_bytes=64) for b in range(1, BLOCKS)]
+        q_c = [keep.tile([P, 2 * P], U32, name="q_c%d" % h, align_bytes=64) for h in range(2)]
+        q_s = [keep.tile([P, 2 * P], U8, name="q_s%d" % h, align_bytes=64) for h in range(2)]
+        y_bf = [q_bf[1][:, 0 : P * PACK], q_bf[1][:, P * PACK : 2 * P * PACK]]
+        y_bf += [keep.tile([P, P * PACK], BF16, name="y_bf%d" % b, align_bytes=64) for b in range(2, BLOCKS)]
         y_c = [keep.tile([P, P], U32, name="y_c%d" % b, align_bytes=64) for b in range(BLOCKS)]
         y_s = [keep.tile([P, P], U8, name="y_s%d" % b, align_bytes=64) for b in range(BLOCKS)]
-        a_ps = [psum.tile([P, PACK, P], F32, name="acc", bufs=6) for b in range(BLOCKS)]
+        a_ps = [psum.tile([P, PACK, P], F32, name="acc", bufs=7) for b in range(BLOCKS)]
 
         def q_cast(h):
             nc.scalar.copy(
@@ -72,19 +75,18 @@ def tile_attend_mlp_relu_topk_kernel(tc, qT, k_words, k_scales, vT, us, offs, ou
             )
 
         def q_quant(h):
-            cols = slice(h * 2 * P, (h + 1) * 2 * P)
-            nc.vector.quantize_mx(out=q_c[:, cols].bitcast(FP8X4), scales=q_s[:, cols], in_=q_bf[h][:])
+            nc.vector.quantize_mx(out=q_c[h][:].bitcast(FP8X4), scales=q_s[h][:], in_=q_bf[h][:])
 
         def first(blocks):
-            for b in blocks:
-                for t in range(PACK):
-                    cols = slice(t * P, (t + 1) * P)
+            for t in range(PACK):
+                cols = slice(t * P, (t + 1) * P)
+                for b in blocks:
                     nc.tensor.matmul_mx(
                         out=a_ps[b][:, t, :],
                         lhsT=kg[:, cols].bitcast(FP8X4),
                         lhsT_scale=ksg[:, cols],
-                        rhs=q_c[:, b * P : (b + 1) * P].bitcast(FP8X4),
-                        rhs_scale=q_s[:, b * P : (b + 1) * P],
+                        rhs=q_c[b // 2][:, (b % 2) * P : (b % 2 + 1) * P].bitcast(FP8X4),
+                        rhs_scale=q_s[b // 2][:, (b % 2) * P : (b % 2 + 1) * P],
                         start=True,
                         stop=True,
                     )
@@ -108,17 +110,16 @@ def tile_attend_mlp_relu_topk_kernel(tc, qT, k_words, k_scales, vT, us, offs, ou
         v_g0 = keep.tile([P, SLOTS], BF16, name="v_g0", align_bytes=64)
         v_half = keep.tile([P, POOL], BF16, name="v_half", align_bytes=64)
         v_g = [v_g0, y_bf[2], y_bf[3], v_bf[1]]
-        v_s = keep.tile([P, DV], U8, name="v_s", align_bytes=64)
 
         def v_gather(c):
-            placed = v_g[c][:].rearrange("p (u m j) -> p m u j", u=2, j=2)
+            placed = v_g[c][:].rearrange("p (u g x) -> p g u x", u=2, x=16)
             if c == 0:
                 nc.scalar.activation(v_half[:], v_raw[c][:], ACT.Copy)
                 nc.scalar.activation(placed, v_half[:].indirect(offsets[:]), ACT.Copy)
             else:
                 nc.vector.tensor_copy(placed, v_raw[c][:].indirect(offsets[:]))
             words = v_g[c][:].bitcast(F32)
-            t_ps = psum.tile([P, 2, P], F32, name="t_ps", bufs=2)
+            t_ps = psum.tile([P, 2, P], F32, name="t_ps", bufs=1)
             for u in range(2):
                 nc.tensor.transpose(t_ps[:, u, :], words[:, u * P : (u + 1) * P], ident[:])
             nc.scalar.copy(
@@ -128,38 +129,54 @@ def tile_attend_mlp_relu_topk_kernel(tc, qT, k_words, k_scales, vT, us, offs, ou
 
         def v_quant(values, e0, ne, tag):
             codes = keep.tile([P, ne], U32, name=tag, align_bytes=64)
-            nc.vector.quantize_mx(out=codes[:].bitcast(FP8X4), scales=v_s[:, e0 : e0 + ne], in_=values)
-            return codes
+            scales = keep.tile([P, ne], U8, name="v_s%d" % e0, align_bytes=64)
+            nc.vector.quantize_mx(out=codes[:].bitcast(FP8X4), scales=scales[:], in_=values)
+            return codes, scales
 
         out_v = out[0].rearrange("(b p) e -> p b e", p=P)
 
-        def second(codes, b0, nb, e0, ne, res, copy):
-            o_ps = psum.tile([P, nb, ne], F32, name="acc", bufs=6)
-            cols = slice(e0, e0 + ne)
-            for b in range(nb):
-                nc.tensor.matmul_mx(
-                    out=o_ps[:, b, :],
-                    lhsT=y_c[b0 + b][:].bitcast(FP8X4),
-                    lhsT_scale=y_s[b0 + b][:],
-                    rhs=codes[:].bitcast(FP8X4),
-                    rhs_scale=v_s[:, cols],
-                    start=True,
-                    stop=True,
-                )
-            copy(res, o_ps[:])
+        def second(codes, e0, ne, banks, engines):
+            per_bank = BLOCKS // banks
+            o_ps = [psum.tile([P, per_bank, ne], F32, name="acc", bufs=7) for bank in range(banks)]
+            for bank in range(banks):
+                for i in range(per_bank):
+                    b = bank * per_bank + i
+                    nc.tensor.matmul_mx(
+                        out=o_ps[bank][:, i, :],
+                        lhsT=y_c[b][:].bitcast(FP8X4),
+                        lhsT_scale=y_s[b][:],
+                        rhs=codes[0][:].bitcast(FP8X4),
+                        rhs_scale=codes[1][:],
+                        start=True,
+                        stop=True,
+                    )
+            for bank in range(banks):
+                copy, queue = engines[bank % len(engines)]
+                res = keep.tile([P, per_bank, ne], F32, name="res_%d_%d" % (e0, bank))
+                copy(res[:], o_ps[bank][:])
+                queue.dma_start(out_v[:, bank * per_bank : (bank + 1) * per_bank, e0 : e0 + ne], res[:])
 
-        res01 = [keep.tile([P, 2, 2 * P], F32, name="res01_%d" % h) for h in range(2)]
-        res2 = keep.tile([P, BLOCKS, P], F32, name="res2")
-        res3 = [keep.tile([P, 2, P], F32, name="res3_%d" % h) for h in range(2)]
+        early = [(nc.scalar.copy, nc.sync)]
+        late = [(nc.vector.tensor_copy, nc.sync), (nc.scalar.copy, nc.scalar)]
 
         q_cast(0)
+        nc.scalar.copy(
+            us_wide[0:1, :].rearrange("o (u j g r) -> o u j g r", u=2, j=2, r=8),
+            us_row[:].rearrange("o (g u r j) -> o u j g r", u=2, j=2, r=8),
+        )
+        us_ps = psum.tile([P, PACK, P], F32, name="t_ps", bufs=1)
+        for t in range(PACK):
+            nc.tensor.transpose(us_ps[:, t, :], us_wide[:, t * P : (t + 1) * P], ident[:])
+        nc.scalar.copy(us_sb[:].rearrange("p o t -> p t o"), us_ps[:, :, 0:1])
         nc.vector.tensor_copy(ksl[:], ks[:].bitcast(U8).indirect(offsets[:]))
         q_quant(0)
         nc.vector.tensor_copy(
-            ksg[:].rearrange("p (t m) -> p t m", t=PACK), ksl[:].rearrange("p (m t) -> p t m", t=PACK)
+            ksg[:].rearrange("p (u j g r) -> p u j g r", u=2, j=2, r=8),
+            ksl[:].rearrange("p (g u r j) -> p u j g r", u=2, j=2, r=8),
         )
         nc.vector.tensor_copy(
-            kg[:].rearrange("p (t m) -> p m t", t=PACK), kw[:].bitcast(U32).indirect(offsets[:])
+            kg[:].rearrange("p (u j g r) -> p g u r j", u=2, j=2, r=8),
+            kw[:].bitcast(U32).indirect(offsets[:]),
         )
         first((0, 1))
         q_cast(1)
@@ -177,15 +194,9 @@ def tile_attend_mlp_relu_topk_kernel(tc, qT, k_words, k_scales, vT, us, offs, ou
         y_quant(3)
         v_gather(2)
         codes01 = v_quant(v_bf01[:], 0, 2 * P, "v_raw2")
-        for h in range(2):
-            second(codes01, 2 * h, 2, 0, 2 * P, res01[h][:], nc.scalar.copy)
-            nc.sync.dma_start(out_v[:, 2 * h : 2 * h + 2, 0 : 2 * P], res01[h][:])
+        second(codes01, 0, 2 * P, 2, early)
         v_gather(3)
         codes2 = v_quant(v_bf[2][:], 2 * P, P, "v_raw3")
-        second(codes2, 0, BLOCKS, 2 * P, P, res2[:], nc.scalar.copy)
-        nc.sync.dma_start(out_v[:, :, 2 * P : 3 * P], res2[:])
+        second(codes2, 2 * P, P, 2, early)
         codes3 = v_quant(v_bf[3][:], 3 * P, P, "codes3")
-        second(codes3, 0, 2, 3 * P, P, res3[0][:], nc.vector.tensor_copy)
-        nc.sync.dma_start(out_v[:, 0:2, 3 * P : DV], res3[0][:])
-        second(codes3, 2, 2, 3 * P, P, res3[1][:], nc.scalar.copy)
-        nc.scalar.dma_start(out_v[:, 2:4, 3 * P : DV], res3[1][:])
+        second(codes3, 3 * P, P, 4, late)

@@ -21,6 +21,7 @@ D = 512
 NQ = 512
 DV = 512
 BLOCKS = 4
+HALF = POOL // 2
 
 FLOPS = 2 * SLOTS * NQ * D + 2 * SLOTS * NQ * DV
 
@@ -34,62 +35,61 @@ def tile_attend_mlp_relu_topk_kernel(tc, qT, k_words, k_scales, vT, us, offs, ou
         offsets = keep.tile([P, SLOTS // 16], U16, name="offsets")
         kw = keep.tile([P, POOL], I32, name="kw", align_bytes=64)
         ks = keep.tile([P, POOL // 4], I32, name="ks", align_bytes=64)
-        q_raw = [keep.tile([P, PACK, NQ // 2], F32, name="q_raw%d" % h, align_bytes=64) for h in range(2)]
-        us_row = keep.tile([1, SLOTS], F32, name="us_row")
-        us_wide = keep.tile([P, SLOTS], F32, name="us_wide", align_bytes=64)
+        q_raw = keep.tile([P, PACK, NQ], F32, name="q_raw", align_bytes=64)
         us_sb = keep.tile([P, 1, PACK], F32, name="us_sb")
-        v_raw = [keep.tile([P, POOL], F32, name="v_raw%d" % c, align_bytes=64) for c in range(BLOCKS)]
+        v_raw = {c: keep.tile([P, POOL], F32, name="v_raw%d" % c, align_bytes=64) for c in range(1, BLOCKS)}
         ident = keep.tile([P, P], F32, name="ident", align_bytes=64)
 
         nc.vector.memset(ks[:], 0)
+        k_rows = k_words[0].rearrange("p t r -> p (t r)").bitcast(I32)
+        nc.sync.dma_start(kw[:, 0:HALF], k_rows[:, 0:HALF])
         nc.sync.dma_start(offsets[:], offs)
-        q_rows = qT[0].rearrange("(p j) w -> p j w", j=PACK)
-        nc.sync.dma_start(q_raw[0][:], q_rows[:, :, 0 : 2 * P])
         for g in range(4):
             nc.sync.dma_start(ks[32 * g : 32 * g + 4, :], k_scales[0, 4 * g : 4 * g + 4, :].bitcast(I32))
-        nc.sync.dma_start(us_row[:], us[0].rearrange("s o -> o s"))
-        nc.sync.dma_start(kw[:], k_words[0].rearrange("p t r -> p (t r)").bitcast(I32))
-        nc.sync.dma_start(q_raw[1][:], q_rows[:, :, 2 * P : NQ])
-        for c in range(BLOCKS):
+        nc.sync.dma_start(kw[:, HALF:POOL], k_rows[:, HALF:POOL])
+        nc.sync.dma_start(q_raw[:], qT[0].rearrange("(p j) w -> p j w", j=PACK))
+        nc.sync.dma_start(us_sb[:], us[0].rearrange("(p t) o -> p o t", t=PACK))
+        v_first = [keep.tile([P, HALF], F32, name="v_first%d" % h, align_bytes=64) for h in range(2)]
+        for h in range(2):
+            nc.sync.dma_start(v_first[h][:], vT[0:P, h * HALF : (h + 1) * HALF])
+        for c in range(1, BLOCKS):
             nc.sync.dma_start(v_raw[c][:], vT[c * P : (c + 1) * P, :])
         make_identity(nc, ident[:])
-        nc.gpsimd.memset(us_wide[:], 0.0)
 
         kg = keep.tile([P, SLOTS], U32, name="kg", align_bytes=64)
         ksl = keep.tile([P, SLOTS], U8, name="ksl", align_bytes=64)
         ksg = keep.tile([P, SLOTS], U8, name="ksg", align_bytes=64)
 
-        q_bf = [keep.tile([P, 2 * P * PACK], BF16, name="q_bf%d" % h, align_bytes=64) for h in range(2)]
-        q_c = [keep.tile([P, 2 * P], U32, name="q_c%d" % h, align_bytes=64) for h in range(2)]
-        q_s = [keep.tile([P, 2 * P], U8, name="q_s%d" % h, align_bytes=64) for h in range(2)]
-        y_bf = [q_bf[1][:, 0 : P * PACK], q_bf[1][:, P * PACK : 2 * P * PACK]]
+        q_bf = [keep.tile([P, P * PACK], BF16, name="q_bf%d" % b, align_bytes=64) for b in range(BLOCKS)]
+        q_c = [keep.tile([P, P], U32, name="q_c%d" % b, align_bytes=64) for b in range(BLOCKS)]
+        q_s = [keep.tile([P, P], U8, name="q_s%d" % b, align_bytes=64) for b in range(BLOCKS)]
+        y_bf = [q_bf[2], q_bf[3]]
         y_bf += [keep.tile([P, P * PACK], BF16, name="y_bf%d" % b, align_bytes=64) for b in range(2, BLOCKS)]
         y_c = [keep.tile([P, P], U32, name="y_c%d" % b, align_bytes=64) for b in range(BLOCKS)]
         y_s = [keep.tile([P, P], U8, name="y_s%d" % b, align_bytes=64) for b in range(BLOCKS)]
-        a_ps = [psum.tile([P, PACK, P], F32, name="acc", bufs=7) for b in range(BLOCKS)]
+        a_ps = [psum.tile([P, PACK, P], F32, name="acc", bufs=6) for b in range(BLOCKS)]
 
-        def q_cast(h):
-            nc.scalar.copy(
-                q_bf[h][:].rearrange("p (w j) -> p w j", j=PACK),
-                q_raw[h][:].rearrange("p j w -> p w j"),
+        def q_cast(b, copy):
+            copy(
+                q_bf[b][:].rearrange("p (c i t) -> p c t i", i=4, t=PACK),
+                q_raw[:, :, b * P : (b + 1) * P].rearrange("p t (c i) -> p c t i", i=4),
             )
 
-        def q_quant(h):
-            nc.vector.quantize_mx(out=q_c[h][:].bitcast(FP8X4), scales=q_s[h][:], in_=q_bf[h][:])
+        def q_quant(b):
+            nc.vector.quantize_mx(out=q_c[b][:].bitcast(FP8X4), scales=q_s[b][:], in_=q_bf[b][:])
 
-        def first(blocks):
+        def first(b):
             for t in range(PACK):
                 cols = slice(t * P, (t + 1) * P)
-                for b in blocks:
-                    nc.tensor.matmul_mx(
-                        out=a_ps[b][:, t, :],
-                        lhsT=kg[:, cols].bitcast(FP8X4),
-                        lhsT_scale=ksg[:, cols],
-                        rhs=q_c[b // 2][:, (b % 2) * P : (b % 2 + 1) * P].bitcast(FP8X4),
-                        rhs_scale=q_s[b // 2][:, (b % 2) * P : (b % 2 + 1) * P],
-                        start=True,
-                        stop=True,
-                    )
+                nc.tensor.matmul_mx(
+                    out=a_ps[b][:, t, :],
+                    lhsT=kg[:, cols].bitcast(FP8X4),
+                    lhsT_scale=ksg[:, cols],
+                    rhs=q_c[b][:].bitcast(FP8X4),
+                    rhs_scale=q_s[b][:],
+                    start=True,
+                    stop=True,
+                )
 
         def y_make(b):
             nc.vector.scalar_tensor_tensor(
@@ -107,21 +107,20 @@ def tile_attend_mlp_relu_topk_kernel(tc, qT, k_words, k_scales, vT, us, offs, ou
         v_bf01 = keep.tile([P, 2 * P * PACK], BF16, name="v_bf01", align_bytes=64)
         v_bf = [v_bf01[:, 0 : P * PACK], v_bf01[:, P * PACK : 2 * P * PACK]]
         v_bf += [keep.tile([P, P * PACK], BF16, name="v_bf%d" % c, align_bytes=64) for c in range(2, BLOCKS)]
-        v_g0 = keep.tile([P, SLOTS], BF16, name="v_g0", align_bytes=64)
+        v_g = [keep.tile([P, SLOTS], BF16, name="v_g%d" % c, align_bytes=64) for c in range(BLOCKS)]
         v_half = keep.tile([P, POOL], BF16, name="v_half", align_bytes=64)
-        v_g = [v_g0, y_bf[2], y_bf[3], v_bf[1]]
 
         def v_gather(c):
-            placed = v_g[c][:].rearrange("p (u g x) -> p g u x", u=2, x=16)
             if c == 0:
-                nc.scalar.activation(v_half[:], v_raw[c][:], ACT.Copy)
-                nc.scalar.activation(placed, v_half[:].indirect(offsets[:]), ACT.Copy)
+                for h in range(2):
+                    nc.scalar.activation(v_half[:, h * HALF : (h + 1) * HALF], v_first[h][:], ACT.Copy)
+                nc.scalar.activation(v_g[c][:], v_half[:].indirect(offsets[:]), ACT.Copy)
             else:
-                nc.vector.tensor_copy(placed, v_raw[c][:].indirect(offsets[:]))
+                nc.vector.tensor_copy(v_g[c][:], v_raw[c][:].indirect(offsets[:]))
             words = v_g[c][:].bitcast(F32)
-            t_ps = psum.tile([P, 2, P], F32, name="t_ps", bufs=1)
+            t_ps = psum.tile([P, 2, P], F32, name="t_ps", bufs=2)
             for u in range(2):
-                nc.tensor.transpose(t_ps[:, u, :], words[:, u * P : (u + 1) * P], ident[:])
+                nc.tensor.transpose(t_ps[:, u, :], words[:, u : 2 * P : 2], ident[:])
             nc.scalar.copy(
                 v_bf[c][:].bitcast(F32).rearrange("p (e u) -> p e u", u=2),
                 t_ps[:].rearrange("p u e -> p e u"),
@@ -137,7 +136,7 @@ def tile_attend_mlp_relu_topk_kernel(tc, qT, k_words, k_scales, vT, us, offs, ou
 
         def second(codes, e0, ne, banks, engines):
             per_bank = BLOCKS // banks
-            o_ps = [psum.tile([P, per_bank, ne], F32, name="acc", bufs=7) for bank in range(banks)]
+            o_ps = [psum.tile([P, per_bank, ne], F32, name="acc", bufs=6) for bank in range(banks)]
             for bank in range(banks):
                 for i in range(per_bank):
                     b = bank * per_bank + i
@@ -159,39 +158,28 @@ def tile_attend_mlp_relu_topk_kernel(tc, qT, k_words, k_scales, vT, us, offs, ou
         early = [(nc.scalar.copy, nc.sync)]
         late = [(nc.vector.tensor_copy, nc.sync), (nc.scalar.copy, nc.scalar)]
 
-        q_cast(0)
-        nc.scalar.copy(
-            us_wide[0:1, :].rearrange("o (u j g r) -> o u j g r", u=2, j=2, r=8),
-            us_row[:].rearrange("o (g u r j) -> o u j g r", u=2, j=2, r=8),
-        )
-        us_ps = psum.tile([P, PACK, P], F32, name="t_ps", bufs=1)
-        for t in range(PACK):
-            nc.tensor.transpose(us_ps[:, t, :], us_wide[:, t * P : (t + 1) * P], ident[:])
-        nc.scalar.copy(us_sb[:].rearrange("p o t -> p t o"), us_ps[:, :, 0:1])
         nc.vector.tensor_copy(ksl[:], ks[:].bitcast(U8).indirect(offsets[:]))
-        q_quant(0)
         nc.vector.tensor_copy(
-            ksg[:].rearrange("p (u j g r) -> p u j g r", u=2, j=2, r=8),
-            ksl[:].rearrange("p (g u r j) -> p u j g r", u=2, j=2, r=8),
+            ksg[:].rearrange("p (t s) -> p t s", t=PACK),
+            ksl[:].rearrange("p (s t) -> p t s", t=PACK),
         )
         nc.vector.tensor_copy(
-            kg[:].rearrange("p (u j g r) -> p g u r j", u=2, j=2, r=8),
+            kg[:].rearrange("p (t s) -> p s t", t=PACK),
             kw[:].bitcast(U32).indirect(offsets[:]),
         )
-        first((0, 1))
-        q_cast(1)
-        q_quant(1)
-        first((2, 3))
+        q_cast(0, nc.vector.tensor_copy)
+        for b in range(1, BLOCKS):
+            q_cast(b, nc.scalar.copy)
+        for b in range(BLOCKS):
+            q_quant(b)
+            first(b)
         y_make(0)
-        y_make(1)
-        y_quant(0)
-        y_make(2)
-        y_quant(1)
-        y_make(3)
-        y_quant(2)
+        for b in range(1, BLOCKS):
+            y_make(b)
+            y_quant(b - 1)
         v_gather(0)
-        v_gather(1)
         y_quant(3)
+        v_gather(1)
         v_gather(2)
         codes01 = v_quant(v_bf01[:], 0, 2 * P, "v_raw2")
         second(codes01, 0, 2 * P, 2, early)

@@ -30,34 +30,30 @@ def tile_attend_mlp_relu_topk_kernel(tc, qT, k_words, k_scales, vT, us, offs, ou
     nc = tc.nc
     with ExitStack() as ctx:
         keep = ctx.enter_context(tc.tile_pool(name="keep", bufs=1))
+        shared = ctx.enter_context(tc.tile_pool(name="shared", bufs=1))
         psum = ctx.enter_context(tc.psum_pool(name="psum", bufs=1))
 
         offsets = keep.tile([P, SLOTS // 16], U16, name="offsets")
-        kw = keep.tile([P, POOL], I32, name="kw", align_bytes=64)
+        kw = shared.tile([P, POOL], I32, name="kw", align_bytes=64, offset=16384)
         ks = keep.tile([P, POOL // 4], I32, name="ks", align_bytes=64)
         q_raw = keep.tile([P, PACK, NQ], F32, name="q_raw", align_bytes=64)
         us_sb = keep.tile([P, 1, PACK], F32, name="us_sb")
-        v_raw = {c: keep.tile([P, POOL], F32, name="v_raw%d" % c, align_bytes=64) for c in range(1, BLOCKS)}
         ident = keep.tile([P, P], F32, name="ident", align_bytes=64)
 
         nc.vector.memset(ks[:], 0)
         k_rows = k_words[0].rearrange("p t r -> p (t r)").bitcast(I32)
         nc.sync.dma_start(kw[:, 0:HALF], k_rows[:, 0:HALF])
         nc.sync.dma_start(offsets[:], offs)
-        for g in range(4):
-            nc.sync.dma_start(ks[32 * g : 32 * g + 4, :], k_scales[0, 4 * g : 4 * g + 4, :].bitcast(I32))
+        nc.sync.dma_start(ks[0:P:8, :], k_scales[0].bitcast(I32))
         nc.sync.dma_start(kw[:, HALF:POOL], k_rows[:, HALF:POOL])
         nc.sync.dma_start(q_raw[:], qT[0].rearrange("(p j) w -> p j w", j=PACK))
         nc.sync.dma_start(us_sb[:], us[0].rearrange("(p t) o -> p o t", t=PACK))
-        v_first = [keep.tile([P, HALF], F32, name="v_first%d" % h, align_bytes=64) for h in range(2)]
-        for h in range(2):
-            nc.sync.dma_start(v_first[h][:], vT[0:P, h * HALF : (h + 1) * HALF])
-        for c in range(1, BLOCKS):
-            nc.sync.dma_start(v_raw[c][:], vT[c * P : (c + 1) * P, :])
+        v_first = [keep.tile([P, HALF], F32, name="v_first0", align_bytes=64)]
+        nc.sync.dma_start(v_first[0][:], vT[0:P, 0:HALF])
         make_identity(nc, ident[:])
 
         kg = keep.tile([P, SLOTS], U32, name="kg", align_bytes=64)
-        ksl = keep.tile([P, SLOTS], U8, name="ksl", align_bytes=64)
+        ksl = shared.tile([P, SLOTS], U8, name="ksl", align_bytes=64, offset=3840)
         ksg = keep.tile([P, SLOTS], U8, name="ksg", align_bytes=64)
 
         q_bf = [keep.tile([P, P * PACK], BF16, name="q_bf%d" % b, align_bytes=64) for b in range(BLOCKS)]
@@ -126,8 +122,11 @@ def tile_attend_mlp_relu_topk_kernel(tc, qT, k_words, k_scales, vT, us, offs, ou
                 t_ps[:].rearrange("p u e -> p e u"),
             )
 
-        def v_quant(values, e0, ne, tag):
-            codes = keep.tile([P, ne], U32, name=tag, align_bytes=64)
+        def v_quant(values, e0, ne, place):
+            if place is None:
+                codes = keep.tile([P, ne], U32, name="v_c%d" % e0, align_bytes=64)
+            else:
+                codes = shared.tile([P, ne], U32, name="v_c%d" % e0, align_bytes=64, offset=place)
             scales = keep.tile([P, ne], U8, name="v_s%d" % e0, align_bytes=64)
             nc.vector.quantize_mx(out=codes[:].bitcast(FP8X4), scales=scales[:], in_=values)
             return codes, scales
@@ -163,10 +162,19 @@ def tile_attend_mlp_relu_topk_kernel(tc, qT, k_words, k_scales, vT, us, offs, ou
             ksg[:].rearrange("p (t s) -> p t s", t=PACK),
             ksl[:].rearrange("p (s t) -> p t s", t=PACK),
         )
+        ksg_words = ksg[:].bitcast(I32)
+        for j in range(1, 4):
+            nc.sync.dma_start(ksg_words[j:P:32, :], ksg_words[8 * j : P : 32, :])
         nc.vector.tensor_copy(
             kg[:].rearrange("p (t s) -> p s t", t=PACK),
             kw[:].bitcast(U32).indirect(offsets[:]),
         )
+        v_first.append(shared.tile([P, HALF], F32, name="v_first1", align_bytes=64, offset=0))
+        nc.sync.dma_start(v_first[1][:], vT[0:P, HALF:POOL])
+        v_raw = {}
+        for c in range(1, BLOCKS):
+            v_raw[c] = shared.tile([P, POOL], F32, name="v_raw%d" % c, align_bytes=64, offset=8192 * c - 4096)
+            nc.sync.dma_start(v_raw[c][:], vT[c * P : (c + 1) * P, :])
         q_cast(0, nc.vector.tensor_copy)
         for b in range(1, BLOCKS):
             q_cast(b, nc.scalar.copy)
@@ -181,10 +189,10 @@ def tile_attend_mlp_relu_topk_kernel(tc, qT, k_words, k_scales, vT, us, offs, ou
         y_quant(3)
         v_gather(1)
         v_gather(2)
-        codes01 = v_quant(v_bf01[:], 0, 2 * P, "v_raw2")
+        codes01 = v_quant(v_bf01[:], 0, 2 * P, 12288)
         second(codes01, 0, 2 * P, 2, early)
         v_gather(3)
-        codes2 = v_quant(v_bf[2][:], 2 * P, P, "v_raw3")
+        codes2 = v_quant(v_bf[2][:], 2 * P, P, 24576)
         second(codes2, 2 * P, P, 2, early)
-        codes3 = v_quant(v_bf[3][:], 3 * P, P, "codes3")
+        codes3 = v_quant(v_bf[3][:], 3 * P, P, None)
         second(codes3, 3 * P, P, 4, late)

@@ -21,7 +21,8 @@ D = 512
 NQ = 512
 DV = 512
 BLOCKS = 4
-HALF = POOL // 2
+KEY_HEAD = 832
+V_HEAD = 832
 
 FLOPS = 2 * SLOTS * NQ * D + 2 * SLOTS * NQ * DV
 
@@ -34,26 +35,27 @@ def tile_attend_mlp_relu_topk_kernel(tc, qT, k_words, k_scales, vT, us, offs, ou
         psum = ctx.enter_context(tc.psum_pool(name="psum", bufs=1))
 
         offsets = keep.tile([P, SLOTS // 16], U16, name="offsets")
-        kw = shared.tile([P, POOL], I32, name="kw", align_bytes=64, offset=16384)
+        kw = shared.tile([P, POOL], I32, name="kw", align_bytes=64, offset=18432)
         ks = keep.tile([P, POOL // 4], I32, name="ks", align_bytes=64)
         q_raw = keep.tile([P, PACK, NQ], F32, name="q_raw", align_bytes=64)
         us_sb = keep.tile([P, 1, PACK], F32, name="us_sb")
         ident = keep.tile([P, P], F32, name="ident", align_bytes=64)
 
         nc.vector.memset(ks[:], 0)
+        nc.vector.memset(ident[:], 0.0)
         k_rows = k_words[0].rearrange("p t r -> p (t r)").bitcast(I32)
-        nc.sync.dma_start(kw[:, 0:HALF], k_rows[:, 0:HALF])
+        nc.sync.dma_start(kw[:, 0:KEY_HEAD], k_rows[:, 0:KEY_HEAD])
         nc.sync.dma_start(offsets[:], offs)
         nc.sync.dma_start(ks[0:P:8, :], k_scales[0].bitcast(I32))
-        nc.sync.dma_start(kw[:, HALF:POOL], k_rows[:, HALF:POOL])
+        nc.sync.dma_start(kw[:, KEY_HEAD:POOL], k_rows[:, KEY_HEAD:POOL])
         nc.sync.dma_start(q_raw[:], qT[0].rearrange("(p j) w -> p j w", j=PACK))
         nc.sync.dma_start(us_sb[:], us[0].rearrange("(p t) o -> p o t", t=PACK))
-        v_first = [keep.tile([P, HALF], F32, name="v_first0", align_bytes=64)]
-        nc.sync.dma_start(v_first[0][:], vT[0:P, 0:HALF])
-        make_identity(nc, ident[:])
+        v_first = [keep.tile([P, V_HEAD], F32, name="v_first0", align_bytes=64)]
+        nc.sync.dma_start(v_first[0][:], vT[0:P, 0:V_HEAD])
+        make_identity(nc, ident[:], nomemset=True)
 
         kg = keep.tile([P, SLOTS], U32, name="kg", align_bytes=64)
-        ksl = shared.tile([P, SLOTS], U8, name="ksl", align_bytes=64, offset=3840)
+        ksl = shared.tile([P, SLOTS], U8, name="ksl", align_bytes=64, offset=4800)
         ksg = keep.tile([P, SLOTS], U8, name="ksg", align_bytes=64)
 
         q_bf = [keep.tile([P, P * PACK], BF16, name="q_bf%d" % b, align_bytes=64) for b in range(BLOCKS)]
@@ -108,8 +110,8 @@ def tile_attend_mlp_relu_topk_kernel(tc, qT, k_words, k_scales, vT, us, offs, ou
 
         def v_gather(c):
             if c == 0:
-                for h in range(2):
-                    nc.scalar.activation(v_half[:, h * HALF : (h + 1) * HALF], v_first[h][:], ACT.Copy)
+                nc.scalar.activation(v_half[:, 0:V_HEAD], v_first[0][:], ACT.Copy)
+                nc.scalar.activation(v_half[:, V_HEAD:POOL], v_first[1][:], ACT.Copy)
                 nc.scalar.activation(v_g[c][:], v_half[:].indirect(offsets[:]), ACT.Copy)
             else:
                 nc.vector.tensor_copy(v_g[c][:], v_raw[c][:].indirect(offsets[:]))
@@ -169,11 +171,11 @@ def tile_attend_mlp_relu_topk_kernel(tc, qT, k_words, k_scales, vT, us, offs, ou
             kg[:].rearrange("p (t s) -> p s t", t=PACK),
             kw[:].bitcast(U32).indirect(offsets[:]),
         )
-        v_first.append(shared.tile([P, HALF], F32, name="v_first1", align_bytes=64, offset=0))
-        nc.sync.dma_start(v_first[1][:], vT[0:P, HALF:POOL])
+        v_first.append(shared.tile([P, POOL - V_HEAD], F32, name="v_first1", align_bytes=64, offset=0))
+        nc.sync.dma_start(v_first[1][:], vT[0:P, V_HEAD:POOL])
         v_raw = {}
         for c in range(1, BLOCKS):
-            v_raw[c] = shared.tile([P, POOL], F32, name="v_raw%d" % c, align_bytes=64, offset=8192 * c - 4096)
+            v_raw[c] = shared.tile([P, POOL], F32, name="v_raw%d" % c, align_bytes=64, offset=8192 * c - 3072)
             nc.sync.dma_start(v_raw[c][:], vT[c * P : (c + 1) * P, :])
         q_cast(0, nc.vector.tensor_copy)
         for b in range(1, BLOCKS):
@@ -189,10 +191,10 @@ def tile_attend_mlp_relu_topk_kernel(tc, qT, k_words, k_scales, vT, us, offs, ou
         y_quant(3)
         v_gather(1)
         v_gather(2)
-        codes01 = v_quant(v_bf01[:], 0, 2 * P, 12288)
+        codes01 = v_quant(v_bf01[:], 0, 2 * P, 13312)
         second(codes01, 0, 2 * P, 2, early)
         v_gather(3)
-        codes2 = v_quant(v_bf[2][:], 2 * P, P, 24576)
+        codes2 = v_quant(v_bf[2][:], 2 * P, P, 26624)
         second(codes2, 2 * P, P, 2, early)
         codes3 = v_quant(v_bf[3][:], 3 * P, P, None)
         second(codes3, 3 * P, P, 4, late)

@@ -34,11 +34,11 @@ def tile_attend_mlp_relu_topk_kernel(tc, qT, k_words, k_scales, vT, us, offs, ou
         shared = ctx.enter_context(tc.tile_pool(name="shared", bufs=1))
         psum = ctx.enter_context(tc.psum_pool(name="psum", bufs=1))
 
-        offsets = keep.tile([P, SLOTS // 16], U16, name="offsets")
-        kw = shared.tile([P, POOL], I32, name="kw", align_bytes=64, offset=18432)
-        ks = keep.tile([P, POOL // 4], I32, name="ks", align_bytes=64)
-        q_raw = keep.tile([P, PACK, NQ], F32, name="q_raw", align_bytes=64)
-        us_sb = keep.tile([P, 1, PACK], F32, name="us_sb")
+        offsets = keep.tile([P, SLOTS // 16], U16, name="offsets", align_bytes=256)
+        kw = shared.tile([P, POOL], I32, name="kw", align_bytes=256, offset=18432)
+        ks = keep.tile([P, POOL // 4], I32, name="ks", align_bytes=256)
+        q_raw = keep.tile([P, PACK, NQ], F32, name="q_raw", align_bytes=256)
+        us_sb = keep.tile([P, 1, PACK], F32, name="us_sb", align_bytes=256)
         ident = keep.tile([P, P], F32, name="ident", align_bytes=64)
 
         nc.vector.memset(ks[:], 0)
@@ -50,13 +50,13 @@ def tile_attend_mlp_relu_topk_kernel(tc, qT, k_words, k_scales, vT, us, offs, ou
         nc.sync.dma_start(kw[:, KEY_HEAD:POOL], k_rows[:, KEY_HEAD:POOL])
         nc.sync.dma_start(q_raw[:], qT[0].rearrange("(p j) w -> p j w", j=PACK))
         nc.sync.dma_start(us_sb[:], us[0].rearrange("(p t) o -> p o t", t=PACK))
-        v_first = [keep.tile([P, V_HEAD], F32, name="v_first0", align_bytes=64)]
+        v_first = [keep.tile([P, V_HEAD], F32, name="v_first0", align_bytes=256)]
         nc.sync.dma_start(v_first[0][:], vT[0:P, 0:V_HEAD])
         make_identity(nc, ident[:], nomemset=True)
 
         kg = keep.tile([P, SLOTS], U32, name="kg", align_bytes=64)
         ksl = shared.tile([P, SLOTS], U8, name="ksl", align_bytes=64, offset=4800)
-        ksg = keep.tile([P, SLOTS], U8, name="ksg", align_bytes=64)
+        ksg = keep.tile([P, SLOTS], U8, name="ksg", align_bytes=256)
 
         q_bf = [keep.tile([P, P * PACK], BF16, name="q_bf%d" % b, align_bytes=64) for b in range(BLOCKS)]
         q_c = [keep.tile([P, P], U32, name="q_c%d" % b, align_bytes=64) for b in range(BLOCKS)]
@@ -135,29 +135,25 @@ def tile_attend_mlp_relu_topk_kernel(tc, qT, k_words, k_scales, vT, us, offs, ou
 
         out_v = out[0].rearrange("(b p) e -> p b e", p=P)
 
-        def second(codes, e0, ne, banks, engines):
+        def second(codes, ne, banks):
             per_bank = BLOCKS // banks
             o_ps = [psum.tile([P, per_bank, ne], F32, name="acc", bufs=6) for bank in range(banks)]
-            for bank in range(banks):
-                for i in range(per_bank):
-                    b = bank * per_bank + i
-                    nc.tensor.matmul_mx(
-                        out=o_ps[bank][:, i, :],
-                        lhsT=y_c[b][:].bitcast(FP8X4),
-                        lhsT_scale=y_s[b][:],
-                        rhs=codes[0][:].bitcast(FP8X4),
-                        rhs_scale=codes[1][:],
-                        start=True,
-                        stop=True,
-                    )
-            for bank in range(banks):
-                copy, queue = engines[bank % len(engines)]
-                res = keep.tile([P, per_bank, ne], F32, name="res_%d_%d" % (e0, bank))
-                copy(res[:], o_ps[bank][:])
-                queue.dma_start(out_v[:, bank * per_bank : (bank + 1) * per_bank, e0 : e0 + ne], res[:])
+            for b in range(BLOCKS):
+                nc.tensor.matmul_mx(
+                    out=o_ps[b // per_bank][:, b % per_bank, :],
+                    lhsT=y_c[b][:].bitcast(FP8X4),
+                    lhsT_scale=y_s[b][:],
+                    rhs=codes[0][:].bitcast(FP8X4),
+                    rhs_scale=codes[1][:],
+                    start=True,
+                    stop=True,
+                )
+            return o_ps
 
-        early = [(nc.scalar.copy, nc.sync)]
-        late = [(nc.vector.tensor_copy, nc.sync), (nc.scalar.copy, nc.scalar)]
+        def leave(bank, b0, nb, e0, ne, copy, queue):
+            res = keep.tile([P, nb, ne], F32, name="res_%d_%d" % (e0, b0), align_bytes=256)
+            copy(res[:], bank[:])
+            queue.dma_start(out_v[:, b0 : b0 + nb, e0 : e0 + ne], res[:])
 
         nc.vector.tensor_copy(ksl[:], ks[:].bitcast(U8).indirect(offsets[:]))
         nc.vector.tensor_copy(
@@ -171,11 +167,11 @@ def tile_attend_mlp_relu_topk_kernel(tc, qT, k_words, k_scales, vT, us, offs, ou
             kg[:].rearrange("p (t s) -> p s t", t=PACK),
             kw[:].bitcast(U32).indirect(offsets[:]),
         )
-        v_first.append(shared.tile([P, POOL - V_HEAD], F32, name="v_first1", align_bytes=64, offset=0))
+        v_first.append(shared.tile([P, POOL - V_HEAD], F32, name="v_first1", align_bytes=256, offset=0))
         nc.sync.dma_start(v_first[1][:], vT[0:P, V_HEAD:POOL])
         v_raw = {}
         for c in range(1, BLOCKS):
-            v_raw[c] = shared.tile([P, POOL], F32, name="v_raw%d" % c, align_bytes=64, offset=8192 * c - 3072)
+            v_raw[c] = shared.tile([P, POOL], F32, name="v_raw%d" % c, align_bytes=256, offset=8192 * c - 3072)
             nc.sync.dma_start(v_raw[c][:], vT[c * P : (c + 1) * P, :])
         q_cast(0, nc.vector.tensor_copy)
         for b in range(1, BLOCKS):
@@ -192,9 +188,16 @@ def tile_attend_mlp_relu_topk_kernel(tc, qT, k_words, k_scales, vT, us, offs, ou
         v_gather(1)
         v_gather(2)
         codes01 = v_quant(v_bf01[:], 0, 2 * P, 13312)
-        second(codes01, 0, 2 * P, 2, early)
+        o01 = second(codes01, 2 * P, 2)
+        leave(o01[0], 0, 2, 0, 2 * P, nc.scalar.copy, nc.sync)
+        leave(o01[1], 2, 2, 0, 2 * P, nc.scalar.copy, nc.sync)
         v_gather(3)
         codes2 = v_quant(v_bf[2][:], 2 * P, P, 26624)
-        second(codes2, 2 * P, P, 2, early)
+        o2 = second(codes2, P, 2)
+        for bank in range(2):
+            leave(o2[bank], 2 * bank, 2, 2 * P, P, nc.scalar.copy, nc.sync)
         codes3 = v_quant(v_bf[3][:], 3 * P, P, None)
-        second(codes3, 3 * P, P, 4, late)
+        o3 = second(codes3, P, 4)
+        late = [(nc.vector.tensor_copy, nc.sync), (nc.scalar.copy, nc.scalar)]
+        for b in range(BLOCKS):
+            leave(o3[b], b, 1, 3 * P, P, *late[b % 2])

@@ -39,7 +39,7 @@ def tile_attend_mlp_relu_topk_kernel(tc, qT, k_words, k_scales, vT, us, offs, ou
         ks = keep.tile([P, POOL // 4], I32, name="ks", align_bytes=256)
         q_raw = keep.tile([P, PACK, NQ], F32, name="q_raw", align_bytes=256)
         us_sb = keep.tile([P, 1, PACK], F32, name="us_sb", align_bytes=256)
-        ident = keep.tile([P, P], F32, name="ident", align_bytes=64)
+        ident = keep.tile([P, P], F32, name="ident", align_bytes=256)
 
         nc.vector.memset(ks[:], 0)
         nc.vector.memset(ident[:], 0.0)
@@ -54,17 +54,17 @@ def tile_attend_mlp_relu_topk_kernel(tc, qT, k_words, k_scales, vT, us, offs, ou
         nc.sync.dma_start(v_first[0][:], vT[0:P, 0:V_HEAD])
         make_identity(nc, ident[:], nomemset=True)
 
-        kg = keep.tile([P, SLOTS], U32, name="kg", align_bytes=64)
+        kg = keep.tile([P, SLOTS], U32, name="kg", align_bytes=256)
         ksl = shared.tile([P, SLOTS], U8, name="ksl", align_bytes=64, offset=4800)
         ksg = keep.tile([P, SLOTS], U8, name="ksg", align_bytes=256)
 
-        q_bf = [keep.tile([P, P * PACK], BF16, name="q_bf%d" % b, align_bytes=64) for b in range(BLOCKS)]
-        q_c = [keep.tile([P, P], U32, name="q_c%d" % b, align_bytes=64) for b in range(BLOCKS)]
-        q_s = [keep.tile([P, P], U8, name="q_s%d" % b, align_bytes=64) for b in range(BLOCKS)]
+        q_bf = [keep.tile([P, P * PACK], BF16, name="q_bf%d" % b, align_bytes=256) for b in range(BLOCKS)]
+        q_c = [keep.tile([P, P], U32, name="q_c%d" % b, align_bytes=256) for b in range(BLOCKS)]
+        q_s = [keep.tile([P, P], U8, name="q_s%d" % b, align_bytes=256) for b in range(BLOCKS)]
         y_bf = [q_bf[2], q_bf[3]]
-        y_bf += [keep.tile([P, P * PACK], BF16, name="y_bf%d" % b, align_bytes=64) for b in range(2, BLOCKS)]
-        y_c = [keep.tile([P, P], U32, name="y_c%d" % b, align_bytes=64) for b in range(BLOCKS)]
-        y_s = [keep.tile([P, P], U8, name="y_s%d" % b, align_bytes=64) for b in range(BLOCKS)]
+        y_bf += [keep.tile([P, P * PACK], BF16, name="y_bf%d" % b, align_bytes=256) for b in range(2, BLOCKS)]
+        y_c = [keep.tile([P, P], U32, name="y_c%d" % b, align_bytes=256) for b in range(BLOCKS)]
+        y_s = [keep.tile([P, P], U8, name="y_s%d" % b, align_bytes=256) for b in range(BLOCKS)]
         a_ps = [psum.tile([P, PACK, P], F32, name="acc", bufs=6) for b in range(BLOCKS)]
 
         def q_cast(b, copy):
@@ -102,11 +102,11 @@ def tile_attend_mlp_relu_topk_kernel(tc, qT, k_words, k_scales, vT, us, offs, ou
         def y_quant(b):
             nc.vector.quantize_mx(out=y_c[b][:].bitcast(FP8X4), scales=y_s[b][:], in_=y_bf[b][:])
 
-        v_bf01 = keep.tile([P, 2 * P * PACK], BF16, name="v_bf01", align_bytes=64)
+        v_bf01 = keep.tile([P, 2 * P * PACK], BF16, name="v_bf01", align_bytes=256)
         v_bf = [v_bf01[:, 0 : P * PACK], v_bf01[:, P * PACK : 2 * P * PACK]]
-        v_bf += [keep.tile([P, P * PACK], BF16, name="v_bf%d" % c, align_bytes=64) for c in range(2, BLOCKS)]
-        v_g = [keep.tile([P, SLOTS], BF16, name="v_g%d" % c, align_bytes=64) for c in range(BLOCKS)]
-        v_half = keep.tile([P, POOL], BF16, name="v_half", align_bytes=64)
+        v_bf += [keep.tile([P, P * PACK], BF16, name="v_bf%d" % c, align_bytes=256) for c in range(2, BLOCKS)]
+        v_g = [keep.tile([P, SLOTS], BF16, name="v_g%d" % c, align_bytes=256) for c in range(BLOCKS)]
+        v_half = keep.tile([P, POOL], BF16, name="v_half", align_bytes=256)
 
         def v_gather(c):
             if c == 0:
@@ -126,10 +126,10 @@ def tile_attend_mlp_relu_topk_kernel(tc, qT, k_words, k_scales, vT, us, offs, ou
 
         def v_quant(values, e0, ne, place):
             if place is None:
-                codes = keep.tile([P, ne], U32, name="v_c%d" % e0, align_bytes=64)
+                codes = keep.tile([P, ne], U32, name="v_c%d" % e0, align_bytes=256)
             else:
-                codes = shared.tile([P, ne], U32, name="v_c%d" % e0, align_bytes=64, offset=place)
-            scales = keep.tile([P, ne], U8, name="v_s%d" % e0, align_bytes=64)
+                codes = shared.tile([P, ne], U32, name="v_c%d" % e0, align_bytes=256, offset=place)
+            scales = keep.tile([P, ne], U8, name="v_s%d" % e0, align_bytes=256)
             nc.vector.quantize_mx(out=codes[:].bitcast(FP8X4), scales=scales[:], in_=values)
             return codes, scales
 
@@ -173,9 +173,8 @@ def tile_attend_mlp_relu_topk_kernel(tc, qT, k_words, k_scales, vT, us, offs, ou
         for c in range(1, BLOCKS):
             v_raw[c] = shared.tile([P, POOL], F32, name="v_raw%d" % c, align_bytes=256, offset=8192 * c - 3072)
             nc.sync.dma_start(v_raw[c][:], vT[c * P : (c + 1) * P, :])
-        q_cast(0, nc.vector.tensor_copy)
-        for b in range(1, BLOCKS):
-            q_cast(b, nc.scalar.copy)
+        for b in range(BLOCKS):
+            q_cast(b, nc.vector.tensor_copy if b < 2 else nc.scalar.copy)
         for b in range(BLOCKS):
             q_quant(b)
             first(b)

@@ -119,10 +119,13 @@ def tile_attend_mlp_relu_topk_kernel(tc, qT, k_words, k_scales, vT, us, offs, ou
             t_ps = psum.tile([P, 2, P], F32, name="t_ps", bufs=2)
             for u in range(2):
                 nc.tensor.transpose(t_ps[:, u, :], words[:, u : 2 * P : 2], ident[:])
-            nc.scalar.copy(
-                v_bf[c][:].bitcast(F32).rearrange("p (e u) -> p e u", u=2),
-                t_ps[:].rearrange("p u e -> p e u"),
-            )
+            turned = v_bf[c][:].bitcast(F32).rearrange("p (e u) -> p e u", u=2)
+            bank = t_ps[:].rearrange("p u e -> p e u")
+            if c == 3:
+                for h in range(2):
+                    nc.vector.tensor_copy(turned[:, 64 * h : 64 * h + 64, :], bank[:, 64 * h : 64 * h + 64, :])
+            else:
+                nc.scalar.copy(turned, bank)
 
         def v_quant(values, e0, ne, place):
             if place is None:
@@ -195,7 +198,16 @@ def tile_attend_mlp_relu_topk_kernel(tc, qT, k_words, k_scales, vT, us, offs, ou
         o2 = second(codes2, P, 2)
         for bank in range(2):
             leave(o2[bank], 2 * bank, 2, 2 * P, P, nc.scalar.copy, nc.sync)
-        codes3 = v_quant(v_bf[3][:], 3 * P, P, None)
+        codes3 = (
+            keep.tile([P, P], U32, name="v_c384", align_bytes=256),
+            keep.tile([P, P], U8, name="v_s384", align_bytes=256),
+        )
+        for h in range(2):
+            nc.vector.quantize_mx(
+                out=codes3[0][:, 64 * h : 64 * h + 64].bitcast(FP8X4),
+                scales=codes3[1][:, 64 * h : 64 * h + 64],
+                in_=v_bf[3][:, 256 * h : 256 * h + 256],
+            )
         o3 = second(codes3, P, 4)
         late = [(nc.vector.tensor_copy, nc.sync), (nc.scalar.copy, nc.scalar)]
         for b in range(BLOCKS):

@@ -21,8 +21,11 @@ D = 512
 NQ = 512
 DV = 512
 BLOCKS = 4
-KEY_HEAD = 832
-V_HEAD = 832
+ROW = 4 * POOL
+KEY_HEAD = 640
+V_HEAD = 576
+VECTOR_SLOTS = 320
+BANK = 2048
 
 FLOPS = 2 * SLOTS * NQ * D + 2 * SLOTS * NQ * DV
 
@@ -35,13 +38,14 @@ def tile_attend_mlp_relu_topk_kernel(tc, qT, k_words, k_scales, vT, us, offs, ou
         psum = ctx.enter_context(tc.psum_pool(name="psum", bufs=1))
 
         offsets = keep.tile([P, SLOTS // 16], U16, name="offsets", align_bytes=256)
-        kw = shared.tile([P, POOL], I32, name="kw", align_bytes=256, offset=18432)
-        ks = keep.tile([P, POOL // 4], I32, name="ks", align_bytes=256)
+        kw = shared.tile([P, POOL], I32, name="kw", align_bytes=256, offset=2 * ROW + ROW // 2)
+        ks = shared.tile([P, POOL // 4], I32, name="ks", align_bytes=256, offset=ROW - POOL // 2)
         q_raw = keep.tile([P, PACK, NQ], F32, name="q_raw", align_bytes=256)
         us_sb = keep.tile([P, 1, PACK], F32, name="us_sb", align_bytes=256)
         ident = keep.tile([P, P], F32, name="ident", align_bytes=256)
 
-        nc.vector.memset(ks[:], 0)
+        nc.vector.memset(ks[:, 0 : POOL // 8], 0)
+        nc.gpsimd.memset(ks[:, POOL // 8 : POOL // 4], 0)
         nc.vector.memset(ident[:], 0.0)
         k_rows = k_words[0].rearrange("p t r -> p (t r)").bitcast(I32)
         nc.sync.dma_start(kw[:, 0:KEY_HEAD], k_rows[:, 0:KEY_HEAD])
@@ -50,22 +54,41 @@ def tile_attend_mlp_relu_topk_kernel(tc, qT, k_words, k_scales, vT, us, offs, ou
         nc.sync.dma_start(kw[:, KEY_HEAD:POOL], k_rows[:, KEY_HEAD:POOL])
         nc.sync.dma_start(q_raw[:], qT[0].rearrange("(p j) w -> p j w", j=PACK))
         nc.sync.dma_start(us_sb[:], us[0].rearrange("(p t) o -> p o t", t=PACK))
-        v_first = [keep.tile([P, V_HEAD], F32, name="v_first0", align_bytes=256)]
-        nc.sync.dma_start(v_first[0][:], vT[0:P, 0:V_HEAD])
+        v_head = keep.tile([P, V_HEAD], F32, name="v_head", align_bytes=256)
+        nc.sync.dma_start(v_head[:], vT[0:P, 0:V_HEAD])
         make_identity(nc, ident[:], nomemset=True)
 
         kg = keep.tile([P, SLOTS], U32, name="kg", align_bytes=256)
-        ksl = shared.tile([P, SLOTS], U8, name="ksl", align_bytes=64, offset=4800)
+        ksl = keep.tile([P, SLOTS], U8, name="ksl", align_bytes=256)
         ksg = keep.tile([P, SLOTS], U8, name="ksg", align_bytes=256)
+        nc.vector.tensor_copy(
+            ksl[:].rearrange("p (t s) -> p s t", t=PACK),
+            ks[:].bitcast(U8).indirect(offsets[:]),
+        )
+        ksl_words = ksl[:].bitcast(I32)
+        ksg_words = ksg[:].bitcast(I32)
+        nc.vector.tensor_copy(ksg_words, ksl_words)
+        for j in range(1, 4):
+            nc.sync.dma_start(ksg_words[j:P:32, :], ksl_words[8 * j : P : 32, :])
+        nc.vector.tensor_copy(
+            kg[:].rearrange("p (t s) -> p s t", t=PACK),
+            kw[:].bitcast(U32).indirect(offsets[:]),
+        )
+        v_raw = []
+        for c in range(BLOCKS):
+            v_raw.append(shared.tile([P, POOL], F32, name="v_raw%d" % c, align_bytes=256, offset=ROW * (c % 3)))
+            first_column = V_HEAD if c == 0 else 0
+            nc.sync.dma_start(v_raw[c][:, first_column:POOL], vT[c * P : (c + 1) * P, first_column:POOL])
 
         q_bf = [keep.tile([P, P * PACK], BF16, name="q_bf%d" % b, align_bytes=256) for b in range(BLOCKS)]
         q_c = [keep.tile([P, P], U32, name="q_c%d" % b, align_bytes=256) for b in range(BLOCKS)]
         q_s = [keep.tile([P, P], U8, name="q_s%d" % b, align_bytes=256) for b in range(BLOCKS)]
-        y_bf = [q_bf[2], q_bf[3]]
-        y_bf += [keep.tile([P, P * PACK], BF16, name="y_bf%d" % b, align_bytes=256) for b in range(2, BLOCKS)]
+        y_bf = [q_bf[2], q_bf[3], keep.tile([P, P * PACK], BF16, name="y_bf2", align_bytes=256)]
+        y_last = keep.tile([P, P * PACK + SLOTS // 2], BF16, name="y_last", align_bytes=256)
+        y_bf.append(y_last[:, 0 : P * PACK])
         y_c = [keep.tile([P, P], U32, name="y_c%d" % b, align_bytes=256) for b in range(BLOCKS)]
         y_s = [keep.tile([P, P], U8, name="y_s%d" % b, align_bytes=256) for b in range(BLOCKS)]
-        a_ps = [psum.tile([P, PACK, P], F32, name="acc", bufs=6) for b in range(BLOCKS)]
+        a_ps = [psum.tile([P, PACK, P], F32, name="a_ps%d" % b, offset=BANK * b) for b in range(BLOCKS)]
 
         def q_cast(b, copy):
             copy(
@@ -73,10 +96,8 @@ def tile_attend_mlp_relu_topk_kernel(tc, qT, k_words, k_scales, vT, us, offs, ou
                 q_raw[:, :, b * P : (b + 1) * P].rearrange("p t (c i) -> p c t i", i=4),
             )
 
-        def q_quant(b):
-            nc.vector.quantize_mx(out=q_c[b][:].bitcast(FP8X4), scales=q_s[b][:], in_=q_bf[b][:])
-
         def first(b):
+            nc.vector.quantize_mx(out=q_c[b][:].bitcast(FP8X4), scales=q_s[b][:], in_=q_bf[b][:])
             for t in range(PACK):
                 cols = slice(t * P, (t + 1) * P)
                 nc.tensor.matmul_mx(
@@ -102,113 +123,107 @@ def tile_attend_mlp_relu_topk_kernel(tc, qT, k_words, k_scales, vT, us, offs, ou
         def y_quant(b):
             nc.vector.quantize_mx(out=y_c[b][:].bitcast(FP8X4), scales=y_s[b][:], in_=y_bf[b][:])
 
-        v_bf01 = keep.tile([P, 2 * P * PACK], BF16, name="v_bf01", align_bytes=256)
-        v_bf = [v_bf01[:, 0 : P * PACK], v_bf01[:, P * PACK : 2 * P * PACK]]
-        v_bf += [keep.tile([P, P * PACK], BF16, name="v_bf%d" % c, align_bytes=256) for c in range(2, BLOCKS)]
-        v_g = [keep.tile([P, SLOTS], BF16, name="v_g%d" % c, align_bytes=256) for c in range(BLOCKS)]
-        v_half = keep.tile([P, POOL], BF16, name="v_half", align_bytes=256)
-
-        def v_gather(c):
-            if c == 0:
-                nc.scalar.activation(v_half[:, 0:V_HEAD], v_first[0][:], ACT.Copy)
-                nc.scalar.activation(v_half[:, V_HEAD:POOL], v_first[1][:], ACT.Copy)
-                nc.scalar.activation(v_g[c][:], v_half[:].indirect(offsets[:]), ACT.Copy)
-            else:
-                nc.vector.tensor_copy(v_g[c][:], v_raw[c][:].indirect(offsets[:]))
-            words = v_g[c][:].bitcast(F32)
-            t_ps = psum.tile([P, 2, P], F32, name="t_ps", bufs=2)
-            for u in range(2):
-                nc.tensor.transpose(t_ps[:, u, :], words[:, u : 2 * P : 2], ident[:])
-            turned = v_bf[c][:].bitcast(F32).rearrange("p (e u) -> p e u", u=2)
-            bank = t_ps[:].rearrange("p u e -> p e u")
-            if c == 3:
-                for h in range(2):
-                    nc.vector.tensor_copy(turned[:, 64 * h : 64 * h + 64, :], bank[:, 64 * h : 64 * h + 64, :])
-            else:
-                nc.scalar.copy(turned, bank)
-
-        def v_quant(values, e0, ne, place):
-            if place is None:
-                codes = keep.tile([P, ne], U32, name="v_c%d" % e0, align_bytes=256)
-            else:
-                codes = shared.tile([P, ne], U32, name="v_c%d" % e0, align_bytes=256, offset=place)
-            scales = keep.tile([P, ne], U8, name="v_s%d" % e0, align_bytes=256)
-            nc.vector.quantize_mx(out=codes[:].bitcast(FP8X4), scales=scales[:], in_=values)
-            return codes, scales
-
-        out_v = out[0].rearrange("(b p) e -> p b e", p=P)
-
-        def second(codes, ne, banks):
-            per_bank = BLOCKS // banks
-            o_ps = [psum.tile([P, per_bank, ne], F32, name="acc", bufs=6) for bank in range(banks)]
-            for b in range(BLOCKS):
-                nc.tensor.matmul_mx(
-                    out=o_ps[b // per_bank][:, b % per_bank, :],
-                    lhsT=y_c[b][:].bitcast(FP8X4),
-                    lhsT_scale=y_s[b][:],
-                    rhs=codes[0][:].bitcast(FP8X4),
-                    rhs_scale=codes[1][:],
-                    start=True,
-                    stop=True,
-                )
-            return o_ps
-
-        def leave(bank, b0, nb, e0, ne, copy, queue):
-            res = keep.tile([P, nb, ne], F32, name="res_%d_%d" % (e0, b0), align_bytes=256)
-            copy(res[:], bank[:])
-            queue.dma_start(out_v[:, b0 : b0 + nb, e0 : e0 + ne], res[:])
-
-        nc.vector.tensor_copy(ksl[:], ks[:].bitcast(U8).indirect(offsets[:]))
-        nc.vector.tensor_copy(
-            ksg[:].rearrange("p (t s) -> p t s", t=PACK),
-            ksl[:].rearrange("p (s t) -> p t s", t=PACK),
-        )
-        ksg_words = ksg[:].bitcast(I32)
-        for j in range(1, 4):
-            nc.sync.dma_start(ksg_words[j:P:32, :], ksg_words[8 * j : P : 32, :])
-        nc.vector.tensor_copy(
-            kg[:].rearrange("p (t s) -> p s t", t=PACK),
-            kw[:].bitcast(U32).indirect(offsets[:]),
-        )
-        v_first.append(shared.tile([P, POOL - V_HEAD], F32, name="v_first1", align_bytes=256, offset=0))
-        nc.sync.dma_start(v_first[1][:], vT[0:P, V_HEAD:POOL])
-        v_raw = {}
-        for c in range(1, BLOCKS):
-            v_raw[c] = shared.tile([P, POOL], F32, name="v_raw%d" % c, align_bytes=256, offset=8192 * c - 3072)
-            nc.sync.dma_start(v_raw[c][:], vT[c * P : (c + 1) * P, :])
         for b in range(BLOCKS):
             q_cast(b, nc.vector.tensor_copy if b < 2 else nc.scalar.copy)
+        nc.scalar.copy(v_raw[0][:, 0:V_HEAD], v_head[:])
         for b in range(BLOCKS):
-            q_quant(b)
             first(b)
         y_make(0)
         for b in range(1, BLOCKS):
             y_make(b)
             y_quant(b - 1)
-        v_gather(0)
-        y_quant(3)
-        v_gather(1)
-        v_gather(2)
-        codes01 = v_quant(v_bf01[:], 0, 2 * P, 13312)
-        o01 = second(codes01, 2 * P, 2)
-        leave(o01[0], 0, 2, 0, 2 * P, nc.scalar.copy, nc.sync)
-        leave(o01[1], 2, 2, 0, 2 * P, nc.scalar.copy, nc.sync)
-        v_gather(3)
-        codes2 = v_quant(v_bf[2][:], 2 * P, P, 26624)
-        o2 = second(codes2, P, 2)
-        for bank in range(2):
-            leave(o2[bank], 2 * bank, 2, 2 * P, P, nc.scalar.copy, nc.sync)
-        codes3 = (
-            keep.tile([P, P], U32, name="v_c384", align_bytes=256),
-            keep.tile([P, P], U8, name="v_s384", align_bytes=256),
-        )
+        y_quant(BLOCKS - 1)
+
+        def place(name, dtype, width, at):
+            return shared.tile([P, width], dtype, name=name, align_bytes=256, offset=at)
+
+        picked = [keep.tile([P, SLOTS], BF16, name="v_g0", align_bytes=256), y_last[:, SLOTS // 2 : SLOTS // 2 + SLOTS]]
+        picked += [place("v_g2", BF16, SLOTS, ROW), keep.tile([P, SLOTS], BF16, name="v_g3", align_bytes=256)]
+        v_bf01 = keep.tile([P, 2 * P * PACK], BF16, name="v_bf01", align_bytes=256)
+        v_bf = [v_bf01[:, 0 : P * PACK], v_bf01[:, P * PACK : 2 * P * PACK]]
+        v_bf += [keep.tile([P, P * PACK], BF16, name="v_bf%d" % c, align_bytes=256) for c in range(2, BLOCKS)]
+        turn_bank = [1, 2, 5, 6]
+
+        def gather(c, vector_slots):
+            cut = vector_slots // 16
+            if cut == 0:
+                nc.scalar.activation(picked[c][:], v_raw[c][:].indirect(offsets[:]), ACT.Copy)
+            else:
+                nc.vector.tensor_copy(picked[c][:, 0:vector_slots], v_raw[c][:].indirect(offsets[:, 0:cut]))
+                nc.scalar.activation(
+                    picked[c][:, vector_slots:SLOTS], v_raw[c][:].indirect(offsets[:, cut : SLOTS // 16]), ACT.Copy
+                )
+            words = picked[c][:].bitcast(F32)
+            t_ps = psum.tile([P, 2, P], F32, name="t_ps%d" % c, offset=BANK * turn_bank[c])
+            for u in range(2):
+                nc.tensor.transpose(t_ps[:, u, :], words[:, u : 2 * P : 2], ident[:])
+            return t_ps
+
+        def turn(c, t_ps, pieces, copy):
+            turned = v_bf[c][:].bitcast(F32).rearrange("p (e u) -> p e u", u=2)
+            bank = t_ps[:].rearrange("p u e -> p e u")
+            ne = P // pieces
+            for h in range(pieces):
+                copy(turned[:, ne * h : ne * (h + 1), :], bank[:, ne * h : ne * (h + 1), :])
+
+        def quantise(values, codes, pieces):
+            width = codes.shape[1]
+            scales = keep.tile([P, width], U8, name="v_s", bufs=3, align_bytes=256)
+            ne = width // pieces
+            for h in range(pieces):
+                nc.vector.quantize_mx(
+                    out=codes[:, ne * h : ne * (h + 1)].bitcast(FP8X4),
+                    scales=scales[:, ne * h : ne * (h + 1)],
+                    in_=values[:, PACK * ne * h : PACK * ne * (h + 1)],
+                )
+            return scales
+
+        def second(codes, scales, banks):
+            per_bank = BLOCKS // len(banks)
+            width = codes.shape[1]
+            sums = [psum.tile([P, per_bank, width], F32, name="o%d_%d" % (width, k), offset=BANK * k) for k in banks]
+            for b in range(BLOCKS):
+                nc.tensor.matmul_mx(
+                    out=sums[b // per_bank][:, b % per_bank, :],
+                    lhsT=y_c[b][:].bitcast(FP8X4),
+                    lhsT_scale=y_s[b][:],
+                    rhs=codes[:].bitcast(FP8X4),
+                    rhs_scale=scales[:],
+                    start=True,
+                    stop=True,
+                )
+            return sums
+
+        out_v = out[0].rearrange("(b p) e -> p b e", p=P)
+
+        turn(0, gather(0, 0), 1, nc.scalar.copy)
+        turn(1, gather(1, SLOTS // 2), 1, nc.scalar.copy)
+        t_ps = gather(2, VECTOR_SLOTS)
+        codes01 = place("v_c01", U32, 2 * P, 2 * ROW)
+        o01 = second(codes01, quantise(v_bf01, codes01, 1), [0, 1, 3, 4])
+        turn(2, t_ps, 1, nc.scalar.copy)
+        t_ps = gather(3, VECTOR_SLOTS)
+        res01 = [
+            shared.tile([P, 2, 2 * P], F32, name="res01_%d" % h, align_bytes=256, offset=2048 * h) for h in range(2)
+        ]
+        nc.vector.tensor_copy(res01[0][:, 0:1, :], o01[0][:])
+        codes2 = place("v_c2", U32, P, 4096)
+        scales2 = quantise(v_bf[2], codes2, 1)
+        for b in range(1, BLOCKS):
+            nc.scalar.copy(res01[b // 2][:, b % 2 : b % 2 + 1, :], o01[b][:])
+            if b % 2 == 1:
+                nc.sync.dma_start(out_v[:, b - 1 : b + 1, 0 : 2 * P], res01[b // 2][:])
+        o2 = second(codes2, scales2, [2, 5])
         for h in range(2):
-            nc.vector.quantize_mx(
-                out=codes3[0][:, 64 * h : 64 * h + 64].bitcast(FP8X4),
-                scales=codes3[1][:, 64 * h : 64 * h + 64],
-                in_=v_bf[3][:, 256 * h : 256 * h + 256],
-            )
-        o3 = second(codes3, P, 4)
-        late = [(nc.vector.tensor_copy, nc.sync), (nc.scalar.copy, nc.scalar)]
+            res2 = keep.tile([P, 2, P], F32, name="res2_%d" % h, align_bytes=256)
+            nc.scalar.copy(res2[:], o2[h][:])
+            nc.sync.dma_start(out_v[:, 2 * h : 2 * h + 2, 2 * P : 3 * P], res2[:])
+        turn(3, t_ps, 2, nc.vector.tensor_copy)
+        codes3 = keep.tile([P, P], U32, name="v_c3", align_bytes=256)
+        o3 = second(codes3, quantise(v_bf[3], codes3, 2), [7, 0, 1, 3])
+        copies = [nc.vector.tensor_copy, nc.scalar.copy]
+        queues = [nc.sync, nc.scalar]
         for b in range(BLOCKS):
-            leave(o3[b], b, 1, 3 * P, P, *late[b % 2])
+            res3 = keep.tile([P, 1, P], F32, name="res3_%d" % b, align_bytes=256)
+            copies[b % 2](res3[:], o3[b][:])
+            queues[b % 2].dma_start(out_v[:, b : b + 1, 3 * P : 4 * P], res3[:])

@@ -44,8 +44,7 @@ def tile_attend_mlp_relu_topk_kernel(tc, qT, k_words, k_scales, vT, us, offs, ou
         us_sb = keep.tile([P, 1, PACK], F32, name="us_sb", align_bytes=256)
         ident = keep.tile([P, P], F32, name="ident", align_bytes=256)
 
-        nc.vector.memset(ks[:, 0 : POOL // 8], 0)
-        nc.gpsimd.memset(ks[:, POOL // 8 : POOL // 4], 0)
+        nc.vector.memset(ks[:], 0)
         nc.vector.memset(ident[:], 0.0)
         k_rows = k_words[0].rearrange("p t r -> p (t r)").bitcast(I32)
         nc.sync.dma_start(kw[:, 0:KEY_HEAD], k_rows[:, 0:KEY_HEAD])

@@ -22,8 +22,8 @@ NQ = 512
 DV = 512
 BLOCKS = 4
 ROW = 4 * POOL
-KEY_HEAD = 640
-V_HEAD = 576
+KEY_HEAD = 768
+V_HEAD = 704
 VECTOR_SLOTS = 320
 BANK = 2048
 

@@ -138,7 +138,7 @@ def tile_attend_mlp_relu_topk_kernel(tc, qT, k_words, k_scales, vT, us, offs, ou
 
         picked = [keep.tile([P, SLOTS], BF16, name="v_g0", align_bytes=256), y_last[:, SLOTS // 2 : SLOTS // 2 + SLOTS]]
         picked += [place("v_g2", BF16, SLOTS, ROW), keep.tile([P, SLOTS], BF16, name="v_g3", align_bytes=256)]
-        v_bf01 = keep.tile([P, 2 * P * PACK], BF16, name="v_bf01", align_bytes=256)
+        v_bf01 = place("v_bf01", BF16, 2 * P * PACK, 3 * ROW + ROW // 2)
         v_bf = [v_bf01[:, 0 : P * PACK], v_bf01[:, P * PACK : 2 * P * PACK]]
         v_bf += [keep.tile([P, P * PACK], BF16, name="v_bf%d" % c, align_bytes=256) for c in range(2, BLOCKS)]
         turn_bank = [1, 2, 5, 6]
@@ -167,7 +167,7 @@ def tile_attend_mlp_relu_topk_kernel(tc, qT, k_words, k_scales, vT, us, offs, ou
 
         def quantise(values, codes, pieces):
             width = codes.shape[1]
-            scales = keep.tile([P, width], U8, name="v_s", bufs=3, align_bytes=256)
+            scales = keep.tile([P, width], U8, name="v_s", bufs=4, align_bytes=256)
             ne = width // pieces
             for h in range(pieces):
                 nc.vector.quantize_mx(
@@ -196,22 +196,39 @@ def tile_attend_mlp_relu_topk_kernel(tc, qT, k_words, k_scales, vT, us, offs, ou
         out_v = out[0].rearrange("(b p) e -> p b e", p=P)
 
         turn(0, gather(0, 0), 1, nc.scalar.copy)
-        turn(1, gather(1, SLOTS // 2), 1, nc.scalar.copy)
+        t_ps = gather(1, SLOTS // 2)
+        codes0 = place("v_c0", U32, P, ROW + 2048)
+        scales0 = quantise(v_bf[0], codes0, 1)
+        early = psum.tile([P, 2, P], F32, name="early", offset=BANK * 7)
+        for b in range(2):
+            nc.tensor.matmul_mx(
+                out=early[:, b, :],
+                lhsT=y_c[b][:].bitcast(FP8X4),
+                lhsT_scale=y_s[b][:],
+                rhs=codes0[:].bitcast(FP8X4),
+                rhs_scale=scales0[:],
+                start=True,
+                stop=True,
+            )
+        turn(1, t_ps, 1, nc.scalar.copy)
         t_ps = gather(2, VECTOR_SLOTS)
         codes01 = place("v_c01", U32, 2 * P, 2 * ROW)
         o01 = second(codes01, quantise(v_bf01, codes01, 1), [0, 1, 3, 4])
+        res_early = shared.tile([P, 2, P], F32, name="res_early", align_bytes=256, offset=3 * ROW + ROW // 2)
+        nc.vector.tensor_copy(res_early[:], early[:])
+        nc.sync.dma_start(out_v[:, 0:2, 0:P], res_early[:])
         turn(2, t_ps, 1, nc.scalar.copy)
         t_ps = gather(3, VECTOR_SLOTS)
-        res01 = [
-            shared.tile([P, 2, 2 * P], F32, name="res01_%d" % h, align_bytes=256, offset=2048 * h) for h in range(2)
-        ]
-        nc.vector.tensor_copy(res01[0][:, 0:1, :], o01[0][:])
+        res1 = shared.tile([P, 2, P], F32, name="res1", align_bytes=256, offset=0)
+        res01 = shared.tile([P, 2, 2 * P], F32, name="res01", align_bytes=256, offset=2048)
+        nc.vector.tensor_copy(res1[:, 0:1, :], o01[0][:, :, P : 2 * P])
+        nc.scalar.copy(res1[:, 1:2, :], o01[1][:, :, P : 2 * P])
+        nc.sync.dma_start(out_v[:, 0:2, P : 2 * P], res1[:])
         codes2 = place("v_c2", U32, P, 4096)
         scales2 = quantise(v_bf[2], codes2, 1)
-        for b in range(1, BLOCKS):
-            nc.scalar.copy(res01[b // 2][:, b % 2 : b % 2 + 1, :], o01[b][:])
-            if b % 2 == 1:
-                nc.sync.dma_start(out_v[:, b - 1 : b + 1, 0 : 2 * P], res01[b // 2][:])
+        nc.vector.tensor_copy(res01[:, 0:1, :], o01[2][:])
+        nc.scalar.copy(res01[:, 1:2, :], o01[3][:])
+        nc.sync.dma_start(out_v[:, 2:4, 0 : 2 * P], res01[:])
         o2 = second(codes2, scales2, [2, 5])
         for h in range(2):
             res2 = keep.tile([P, 2, P], F32, name="res2_%d" % h, align_bytes=256)

@@ -52,7 +52,7 @@ def tile_attend_mlp_relu_topk_kernel(tc, qT, k_words, k_scales, vT, us, offs, ou
         nc.sync.dma_start(ks[0:P:8, :], k_scales[0].bitcast(I32))
         nc.sync.dma_start(kw[:, KEY_HEAD:POOL], k_rows[:, KEY_HEAD:POOL])
         nc.sync.dma_start(q_raw[:], qT[0].rearrange("(p j) w -> p j w", j=PACK))
-        nc.sync.dma_start(us_sb[:], us[0].rearrange("(p t) o -> p o t", t=PACK))
+        nc.scalar.dma_start(us_sb[:], us[0].rearrange("(p t) o -> p o t", t=PACK))
         v_head = keep.tile([P, V_HEAD], F32, name="v_head", align_bytes=256)
         nc.sync.dma_start(v_head[:], vT[0:P, 0:V_HEAD])
         make_identity(nc, ident[:], nomemset=True)
@@ -79,14 +79,21 @@ def tile_attend_mlp_relu_topk_kernel(tc, qT, k_words, k_scales, vT, us, offs, ou
             first_column = V_HEAD if c == 0 else 0
             nc.sync.dma_start(v_raw[c][:, first_column:POOL], vT[c * P : (c + 1) * P, first_column:POOL])
 
-        q_bf = [keep.tile([P, P * PACK], BF16, name="q_bf%d" % b, align_bytes=256) for b in range(BLOCKS)]
-        q_c = [keep.tile([P, P], U32, name="q_c%d" % b, align_bytes=256) for b in range(BLOCKS)]
-        q_s = [keep.tile([P, P], U8, name="q_s%d" % b, align_bytes=256) for b in range(BLOCKS)]
-        y_bf = [q_bf[2], q_bf[3], keep.tile([P, P * PACK], BF16, name="y_bf2", align_bytes=256)]
-        y_last = keep.tile([P, P * PACK + SLOTS // 2], BF16, name="y_last", align_bytes=256)
-        y_bf.append(y_last[:, 0 : P * PACK])
-        y_c = [keep.tile([P, P], U32, name="y_c%d" % b, align_bytes=256) for b in range(BLOCKS)]
-        y_s = [keep.tile([P, P], U8, name="y_s%d" % b, align_bytes=256) for b in range(BLOCKS)]
+        wide = P * PACK
+        q_pair = keep.tile([P, 2 * wide], BF16, name="q_pair", align_bytes=256)
+        q_bf = [keep.tile([P, wide], BF16, name="q_bf%d" % b, align_bytes=256) for b in range(2)]
+        q_bf += [q_pair[:, 0:wide], q_pair[:, wide : 2 * wide]]
+        q_codes = keep.tile([P, NQ], U32, name="q_codes", align_bytes=256)
+        q_scales = keep.tile([P, NQ], U8, name="q_scales", align_bytes=256)
+        q_c = [q_codes[:, b * P : (b + 1) * P] for b in range(BLOCKS)]
+        q_s = [q_scales[:, b * P : (b + 1) * P] for b in range(BLOCKS)]
+        y_last = keep.tile([P, 2 * wide + SLOTS // 2], BF16, name="y_last", align_bytes=256)
+        y_pair = [q_pair[:], y_last[:, 0 : 2 * wide]]
+        y_bf = [y_pair[b // 2][:, (b % 2) * wide : (b % 2 + 1) * wide] for b in range(BLOCKS)]
+        y_codes = keep.tile([P, NQ], U32, name="y_codes", align_bytes=256)
+        y_scales = keep.tile([P, NQ], U8, name="y_scales", align_bytes=256)
+        y_c = [y_codes[:, b * P : (b + 1) * P] for b in range(BLOCKS)]
+        y_s = [y_scales[:, b * P : (b + 1) * P] for b in range(BLOCKS)]
         a_ps = [psum.tile([P, PACK, P], F32, name="a_ps%d" % b, offset=BANK * b) for b in range(BLOCKS)]
 
         def q_cast(b, copy):
@@ -96,7 +103,11 @@ def tile_attend_mlp_relu_topk_kernel(tc, qT, k_words, k_scales, vT, us, offs, ou
             )
 
         def first(b):
-            nc.vector.quantize_mx(out=q_c[b][:].bitcast(FP8X4), scales=q_s[b][:], in_=q_bf[b][:])
+            if b < 2:
+                nc.vector.quantize_mx(out=q_c[b][:].bitcast(FP8X4), scales=q_s[b][:], in_=q_bf[b][:])
+            if b == 2:
+                half = slice(2 * P, NQ)
+                nc.vector.quantize_mx(out=q_codes[:, half].bitcast(FP8X4), scales=q_scales[:, half], in_=q_pair[:])
             for t in range(PACK):
                 cols = slice(t * P, (t + 1) * P)
                 nc.tensor.matmul_mx(
@@ -119,24 +130,25 @@ def tile_attend_mlp_relu_topk_kernel(tc, qT, k_words, k_scales, vT, us, offs, ou
                 op1=ALU.mult,
             )
 
-        def y_quant(b):
-            nc.vector.quantize_mx(out=y_c[b][:].bitcast(FP8X4), scales=y_s[b][:], in_=y_bf[b][:])
+        def y_quant(h):
+            half = slice(2 * P * h, 2 * P * (h + 1))
+            nc.vector.quantize_mx(out=y_codes[:, half].bitcast(FP8X4), scales=y_scales[:, half], in_=y_pair[h])
 
         for b in range(BLOCKS):
             q_cast(b, nc.vector.tensor_copy if b < 2 else nc.scalar.copy)
         nc.scalar.copy(v_raw[0][:, 0:V_HEAD], v_head[:])
         for b in range(BLOCKS):
             first(b)
-        y_make(0)
-        for b in range(1, BLOCKS):
+        for b in range(3):
             y_make(b)
-            y_quant(b - 1)
-        y_quant(BLOCKS - 1)
+        y_quant(0)
+        y_make(3)
+        y_quant(1)
 
         def place(name, dtype, width, at):
             return shared.tile([P, width], dtype, name=name, align_bytes=256, offset=at)
 
-        picked = [keep.tile([P, SLOTS], BF16, name="v_g0", align_bytes=256), y_last[:, SLOTS // 2 : SLOTS // 2 + SLOTS]]
+        picked = [keep.tile([P, SLOTS], BF16, name="v_g0", align_bytes=256), y_last[:, 2 * wide - SLOTS // 2 : 2 * wide + SLOTS // 2]]
         picked += [place("v_g2", BF16, SLOTS, ROW), keep.tile([P, SLOTS], BF16, name="v_g3", align_bytes=256)]
         v_bf01 = place("v_bf01", BF16, 2 * P * PACK, 3 * ROW + ROW // 2)
         v_bf = [v_bf01[:, 0 : P * PACK], v_bf01[:, P * PACK : 2 * P * PACK]]
@@ -226,8 +238,8 @@ def tile_attend_mlp_relu_topk_kernel(tc, qT, k_words, k_scales, vT, us, offs, ou
         nc.sync.dma_start(out_v[:, 0:2, P : 2 * P], res1[:])
         codes2 = place("v_c2", U32, P, 4096)
         scales2 = quantise(v_bf[2], codes2, 1)
-        nc.vector.tensor_copy(res01[:, 0:1, :], o01[2][:])
-        nc.scalar.copy(res01[:, 1:2, :], o01[3][:])
+        for b in range(2, BLOCKS):
+            nc.scalar.copy(res01[:, b - 2 : b - 1, :], o01[b][:])
         nc.sync.dma_start(out_v[:, 2:4, 0 : 2 * P], res01[:])
         o2 = second(codes2, scales2, [2, 5])
         for h in range(2):

@@ -211,8 +211,8 @@ def tile_attend_mlp_relu_topk_kernel(tc, qT, k_words, k_scales, vT, us, offs, ou
         t_ps = gather(1, SLOTS // 2)
         codes0 = place("v_c0", U32, P, ROW + 2048)
         scales0 = quantise(v_bf[0], codes0, 1)
-        early = psum.tile([P, 2, P], F32, name="early", offset=BANK * 7)
-        for b in range(2):
+        early = psum.tile([P, 3, P], F32, name="early", offset=BANK * 7)
+        for b in range(3):
             nc.tensor.matmul_mx(
                 out=early[:, b, :],
                 lhsT=y_c[b][:].bitcast(FP8X4),
@@ -224,23 +224,23 @@ def tile_attend_mlp_relu_topk_kernel(tc, qT, k_words, k_scales, vT, us, offs, ou
             )
         turn(1, t_ps, 1, nc.scalar.copy)
         t_ps = gather(2, VECTOR_SLOTS)
+        res_early = shared.tile([P, 3, P], F32, name="res_early", align_bytes=256, offset=2 * ROW + 2048)
+        nc.scalar.copy(res_early[:], early[:])
+        nc.sync.dma_start(out_v[:, 0:3, 0:P], res_early[:])
         codes01 = place("v_c01", U32, 2 * P, 2 * ROW)
         o01 = second(codes01, quantise(v_bf01, codes01, 1), [0, 1, 3, 4])
-        res_early = shared.tile([P, 2, P], F32, name="res_early", align_bytes=256, offset=3 * ROW + ROW // 2)
-        nc.vector.tensor_copy(res_early[:], early[:])
-        nc.sync.dma_start(out_v[:, 0:2, 0:P], res_early[:])
         turn(2, t_ps, 1, nc.scalar.copy)
         t_ps = gather(3, VECTOR_SLOTS)
-        res1 = shared.tile([P, 2, P], F32, name="res1", align_bytes=256, offset=0)
-        res01 = shared.tile([P, 2, 2 * P], F32, name="res01", align_bytes=256, offset=2048)
+        res1 = shared.tile([P, 3, P], F32, name="res1", align_bytes=256, offset=0)
+        res01 = shared.tile([P, 1, 2 * P], F32, name="res01", align_bytes=256, offset=2048)
         nc.vector.tensor_copy(res1[:, 0:1, :], o01[0][:, :, P : 2 * P])
-        nc.scalar.copy(res1[:, 1:2, :], o01[1][:, :, P : 2 * P])
-        nc.sync.dma_start(out_v[:, 0:2, P : 2 * P], res1[:])
+        for b in range(1, 3):
+            nc.scalar.copy(res1[:, b : b + 1, :], o01[b][:, :, P : 2 * P])
+        nc.sync.dma_start(out_v[:, 0:3, P : 2 * P], res1[:])
         codes2 = place("v_c2", U32, P, 4096)
         scales2 = quantise(v_bf[2], codes2, 1)
-        for b in range(2, BLOCKS):
-            nc.scalar.copy(res01[:, b - 2 : b - 1, :], o01[b][:])
-        nc.sync.dma_start(out_v[:, 2:4, 0 : 2 * P], res01[:])
+        nc.vector.tensor_copy(res01[:], o01[3][:])
+        nc.sync.dma_start(out_v[:, 3:4, 0 : 2 * P], res01[:])
         o2 = second(codes2, scales2, [2, 5])
         for h in range(2):
             res2 = keep.tile([P, 2, P], F32, name="res2_%d" % h, align_bytes=256)

@@ -230,7 +230,7 @@ def tile_attend_mlp_relu_topk_kernel(tc, qT, k_words, k_scales, vT, us, offs, ou
         codes01 = place("v_c01", U32, 2 * P, 2 * ROW)
         o01 = second(codes01, quantise(v_bf01, codes01, 1), [0, 1, 3, 4])
         turn(2, t_ps, 1, nc.scalar.copy)
-        t_ps = gather(3, VECTOR_SLOTS)
+        t_ps = gather(3, SLOTS // 2)
         res1 = shared.tile([P, 3, P], F32, name="res1", align_bytes=256, offset=0)
         res01 = shared.tile([P, 1, 2 * P], F32, name="res01", align_bytes=256, offset=2048)
         nc.vector.tensor_copy(res1[:, 0:1, :], o01[0][:, :, P : 2 * P])

@@ -150,8 +150,7 @@ def tile_attend_mlp_relu_topk_kernel(tc, qT, k_words, k_scales, vT, us, offs, ou
 
         picked = [keep.tile([P, SLOTS], BF16, name="v_g0", align_bytes=256), y_last[:, 2 * wide - SLOTS // 2 : 2 * wide + SLOTS // 2]]
         picked += [place("v_g2", BF16, SLOTS, ROW), keep.tile([P, SLOTS], BF16, name="v_g3", align_bytes=256)]
-        v_bf01 = place("v_bf01", BF16, 2 * P * PACK, 3 * ROW + ROW // 2)
-        v_bf = [v_bf01[:, 0 : P * PACK], v_bf01[:, P * PACK : 2 * P * PACK]]
+        v_bf = [place("v_bf0", BF16, P * PACK, 3 * ROW + ROW // 2), place("v_bf1", BF16, P * PACK, 2 * ROW)]
         v_bf += [keep.tile([P, P * PACK], BF16, name="v_bf%d" % c, align_bytes=256) for c in range(2, BLOCKS)]
         turn_bank = [1, 2, 5, 6]
 
@@ -177,17 +176,14 @@ def tile_attend_mlp_relu_topk_kernel(tc, qT, k_words, k_scales, vT, us, offs, ou
             for h in range(pieces):
                 copy(turned[:, ne * h : ne * (h + 1), :], bank[:, ne * h : ne * (h + 1), :])
 
-        def quantise(values, codes, pieces):
-            width = codes.shape[1]
-            scales = keep.tile([P, width], U8, name="v_s", bufs=4, align_bytes=256)
-            ne = width // pieces
+        def quantise(values, codes, scales, pieces):
+            ne = codes.shape[1] // pieces
             for h in range(pieces):
                 nc.vector.quantize_mx(
                     out=codes[:, ne * h : ne * (h + 1)].bitcast(FP8X4),
                     scales=scales[:, ne * h : ne * (h + 1)],
                     in_=values[:, PACK * ne * h : PACK * ne * (h + 1)],
                 )
-            return scales
 
         def second(codes, scales, banks):
             per_bank = BLOCKS // len(banks)
@@ -209,26 +205,28 @@ def tile_attend_mlp_relu_topk_kernel(tc, qT, k_words, k_scales, vT, us, offs, ou
 
         turn(0, gather(0, 0), 1, nc.scalar.copy)
         t_ps = gather(1, SLOTS // 2)
-        codes0 = place("v_c0", U32, P, ROW + 2048)
-        scales0 = quantise(v_bf[0], codes0, 1)
+        codes01 = place("v_c01", U32, 2 * P, ROW + 2048)
+        scales01 = keep.tile([P, 2 * P], U8, name="v_s01", align_bytes=256)
+        quantise(v_bf[0], codes01[:, 0:P], scales01[:, 0:P], 1)
         early = psum.tile([P, 3, P], F32, name="early", offset=BANK * 7)
         for b in range(3):
             nc.tensor.matmul_mx(
                 out=early[:, b, :],
                 lhsT=y_c[b][:].bitcast(FP8X4),
                 lhsT_scale=y_s[b][:],
-                rhs=codes0[:].bitcast(FP8X4),
-                rhs_scale=scales0[:],
+                rhs=codes01[:, 0:P].bitcast(FP8X4),
+                rhs_scale=scales01[:, 0:P],
                 start=True,
                 stop=True,
             )
-        turn(1, t_ps, 1, nc.scalar.copy)
+        t_ps1 = t_ps
         t_ps = gather(2, VECTOR_SLOTS)
+        turn(1, t_ps1, 1, nc.scalar.copy)
         res_early = shared.tile([P, 3, P], F32, name="res_early", align_bytes=256, offset=2 * ROW + 2048)
         nc.scalar.copy(res_early[:], early[:])
         nc.sync.dma_start(out_v[:, 0:3, 0:P], res_early[:])
-        codes01 = place("v_c01", U32, 2 * P, 2 * ROW)
-        o01 = second(codes01, quantise(v_bf01, codes01, 1), [0, 1, 3, 4])
+        quantise(v_bf[1], codes01[:, P : 2 * P], scales01[:, P : 2 * P], 1)
+        o01 = second(codes01, scales01, [0, 1, 3, 4])
         turn(2, t_ps, 1, nc.scalar.copy)
         t_ps = gather(3, SLOTS // 2)
         res1 = shared.tile([P, 3, P], F32, name="res1", align_bytes=256, offset=0)
@@ -238,7 +236,8 @@ def tile_attend_mlp_relu_topk_kernel(tc, qT, k_words, k_scales, vT, us, offs, ou
             nc.scalar.copy(res1[:, b : b + 1, :], o01[b][:, :, P : 2 * P])
         nc.sync.dma_start(out_v[:, 0:3, P : 2 * P], res1[:])
         codes2 = place("v_c2", U32, P, 4096)
-        scales2 = quantise(v_bf[2], codes2, 1)
+        scales2 = keep.tile([P, P], U8, name="v_s2", align_bytes=256)
+        quantise(v_bf[2], codes2, scales2, 1)
         nc.vector.tensor_copy(res01[:], o01[3][:])
         nc.sync.dma_start(out_v[:, 3:4, 0 : 2 * P], res01[:])
         o2 = second(codes2, scales2, [2, 5])
@@ -248,7 +247,9 @@ def tile_attend_mlp_relu_topk_kernel(tc, qT, k_words, k_scales, vT, us, offs, ou
             nc.sync.dma_start(out_v[:, 2 * h : 2 * h + 2, 2 * P : 3 * P], res2[:])
         turn(3, t_ps, 2, nc.vector.tensor_copy)
         codes3 = keep.tile([P, P], U32, name="v_c3", align_bytes=256)
-        o3 = second(codes3, quantise(v_bf[3], codes3, 2), [7, 0, 1, 3])
+        scales3 = keep.tile([P, P], U8, name="v_s3", align_bytes=256)
+        quantise(v_bf[3], codes3, scales3, 2)
+        o3 = second(codes3, scales3, [7, 0, 1, 3])
         copies = [nc.vector.tensor_copy, nc.scalar.copy]
         queues = [nc.sync, nc.scalar]
         for b in range(BLOCKS):

@@ -24,7 +24,7 @@ BLOCKS = 4
 ROW = 4 * POOL
 KEY_HEAD = 768
 V_HEAD = 704
-VECTOR_SLOTS = 320
+VECTOR_SLOTS = 288
 BANK = 2048
 
 FLOPS = 2 * SLOTS * NQ * D + 2 * SLOTS * NQ * DV
@@ -220,7 +220,7 @@ def tile_attend_mlp_relu_topk_kernel(tc, qT, k_words, k_scales, vT, us, offs, ou
                 stop=True,
             )
         t_ps1 = t_ps
-        t_ps = gather(2, VECTOR_SLOTS)
+        t_ps = gather(2, SLOTS // 2)
         turn(1, t_ps1, 1, nc.scalar.copy)
         res_early = shared.tile([P, 3, P], F32, name="res_early", align_bytes=256, offset=2 * ROW + 2048)
         nc.scalar.copy(res_early[:], early[:])
@@ -228,18 +228,19 @@ def tile_attend_mlp_relu_topk_kernel(tc, qT, k_words, k_scales, vT, us, offs, ou
         quantise(v_bf[1], codes01[:, P : 2 * P], scales01[:, P : 2 * P], 1)
         o01 = second(codes01, scales01, [0, 1, 3, 4])
         turn(2, t_ps, 1, nc.scalar.copy)
-        t_ps = gather(3, SLOTS // 2)
+        t_ps = gather(3, VECTOR_SLOTS)
         res1 = shared.tile([P, 3, P], F32, name="res1", align_bytes=256, offset=0)
         res01 = shared.tile([P, 1, 2 * P], F32, name="res01", align_bytes=256, offset=2048)
-        nc.vector.tensor_copy(res1[:, 0:1, :], o01[0][:, :, P : 2 * P])
-        for b in range(1, 3):
-            nc.scalar.copy(res1[:, b : b + 1, :], o01[b][:, :, P : 2 * P])
-        nc.sync.dma_start(out_v[:, 0:3, P : 2 * P], res1[:])
         codes2 = place("v_c2", U32, P, 4096)
         scales2 = keep.tile([P, P], U8, name="v_s2", align_bytes=256)
         quantise(v_bf[2], codes2, scales2, 1)
+        nc.scalar.copy(res1[:, 0:1, :], o01[0][:, :, P : 2 * P])
+        nc.sync.dma_start(out_v[:, 0:1, P : 2 * P], res1[:, 0:1, :])
         nc.vector.tensor_copy(res01[:], o01[3][:])
         nc.sync.dma_start(out_v[:, 3:4, 0 : 2 * P], res01[:])
+        for b in range(1, 3):
+            nc.scalar.copy(res1[:, b : b + 1, :], o01[b][:, :, P : 2 * P])
+        nc.sync.dma_start(out_v[:, 1:3, P : 2 * P], res1[:, 1:3, :])
         o2 = second(codes2, scales2, [2, 5])
         for h in range(2):
             res2 = keep.tile([P, 2, P], F32, name="res2_%d" % h, align_bytes=256)

@@ -235,7 +235,7 @@ def tile_attend_mlp_relu_topk_kernel(tc, qT, k_words, k_scales, vT, us, offs, ou
         scales2 = keep.tile([P, P], U8, name="v_s2", align_bytes=256)
         quantise(v_bf[2], codes2, scales2, 1)
         nc.scalar.copy(res1[:, 0:1, :], o01[0][:, :, P : 2 * P])
-        nc.sync.dma_start(out_v[:, 0:1, P : 2 * P], res1[:, 0:1, :])
+        nc.scalar.dma_start(out_v[:, 0:1, P : 2 * P], res1[:, 0:1, :])
         nc.vector.tensor_copy(res01[:], o01[3][:])
         nc.sync.dma_start(out_v[:, 3:4, 0 : 2 * P], res01[:])
         for b in range(1, 3):

@@ -24,6 +24,7 @@ BLOCKS = 4
 ROW = 4 * POOL
 KEY_HEAD = 768
 V_HEAD = 704
+LAST_HEAD = 128
 VECTOR_SLOTS = 288
 BANK = 2048
 
@@ -77,6 +78,9 @@ def tile_attend_mlp_relu_topk_kernel(tc, qT, k_words, k_scales, vT, us, offs, ou
         for c in range(BLOCKS):
             v_raw.append(shared.tile([P, POOL], F32, name="v_raw%d" % c, align_bytes=256, offset=ROW * (c % 3)))
             first_column = V_HEAD if c == 0 else 0
+            if c == BLOCKS - 1:
+                first_column = LAST_HEAD
+                nc.sync.dma_start(v_raw[c][:, 0:LAST_HEAD], vT[c * P : (c + 1) * P, 0:LAST_HEAD])
             nc.sync.dma_start(v_raw[c][:, first_column:POOL], vT[c * P : (c + 1) * P, first_column:POOL])
 
         wide = P * PACK
@@ -234,18 +238,16 @@ def tile_attend_mlp_relu_topk_kernel(tc, qT, k_words, k_scales, vT, us, offs, ou
         codes2 = place("v_c2", U32, P, 4096)
         scales2 = keep.tile([P, P], U8, name="v_s2", align_bytes=256)
         quantise(v_bf[2], codes2, scales2, 1)
-        nc.scalar.copy(res1[:, 0:1, :], o01[0][:, :, P : 2 * P])
-        nc.scalar.dma_start(out_v[:, 0:1, P : 2 * P], res1[:, 0:1, :])
         nc.vector.tensor_copy(res01[:], o01[3][:])
         nc.sync.dma_start(out_v[:, 3:4, 0 : 2 * P], res01[:])
-        for b in range(1, 3):
+        for b in range(3):
             nc.scalar.copy(res1[:, b : b + 1, :], o01[b][:, :, P : 2 * P])
-        nc.sync.dma_start(out_v[:, 1:3, P : 2 * P], res1[:, 1:3, :])
+        nc.sync.dma_start(out_v[:, 0:3, P : 2 * P], res1[:])
         o2 = second(codes2, scales2, [2, 5])
-        for h in range(2):
+        for h, queue in enumerate([nc.sync, nc.scalar]):
             res2 = keep.tile([P, 2, P], F32, name="res2_%d" % h, align_bytes=256)
             nc.scalar.copy(res2[:], o2[h][:])
-            nc.sync.dma_start(out_v[:, 2 * h : 2 * h + 2, 2 * P : 3 * P], res2[:])
+            queue.dma_start(out_v[:, 2 * h : 2 * h + 2, 2 * P : 3 * P], res2[:])
         turn(3, t_ps, 2, nc.vector.tensor_copy)
         codes3 = keep.tile([P, P], U32, name="v_c3", align_bytes=256)
         scales3 = keep.tile([P, P], U8, name="v_s3", align_bytes=256)

from contextlib import ExitStack

import concourse.mybir as mybir
from concourse.masks import make_identity

F32 = mybir.dt.float32
BF16 = mybir.dt.bfloat16
I32 = mybir.dt.int32
U32 = mybir.dt.uint32
U16 = mybir.dt.uint16
U8 = mybir.dt.uint8
FP8X4 = mybir.dt.float8_e4m3fn_x4
ALU = mybir.AluOpType
ACT = mybir.ActivationFunctionType

P = 128
PACK = 4
SLOTS = 512
POOL = 2048
D = 512
NQ = 512
DV = 512
BLOCKS = 4
ROW = 4 * POOL
KEY_HEAD = 768
V_HEAD = 704
LAST_HEAD = 128
VECTOR_SLOTS = 288
BANK = 2048

FLOPS = 2 * SLOTS * NQ * D + 2 * SLOTS * NQ * DV


def tile_attend_mlp_relu_topk_kernel(tc, qT, k_words, k_scales, vT, us, offs, out):
    nc = tc.nc
    with ExitStack() as ctx:
        keep = ctx.enter_context(tc.tile_pool(name="keep", bufs=1))
        shared = ctx.enter_context(tc.tile_pool(name="shared", bufs=1))
        psum = ctx.enter_context(tc.psum_pool(name="psum", bufs=1))

        offsets = keep.tile([P, SLOTS // 16], U16, name="offsets", align_bytes=256)
        kw = shared.tile([P, POOL], I32, name="kw", align_bytes=256, offset=2 * ROW + ROW // 2)
        ks = shared.tile([P, POOL // 4], I32, name="ks", align_bytes=256, offset=ROW - POOL // 2)
        q_raw = keep.tile([P, PACK, NQ], F32, name="q_raw", align_bytes=256)
        us_sb = keep.tile([P, 1, PACK], F32, name="us_sb", align_bytes=256)
        ident = keep.tile([P, P], F32, name="ident", align_bytes=256)

        nc.vector.memset(ks[:], 0)
        nc.vector.memset(ident[:], 0.0)
        k_rows = k_words[0].rearrange("p t r -> p (t r)").bitcast(I32)
        nc.sync.dma_start(kw[:, 0:KEY_HEAD], k_rows[:, 0:KEY_HEAD])
        nc.sync.dma_start(offsets[:], offs)
        nc.sync.dma_start(ks[0:P:8, :], k_scales[0].bitcast(I32))
        nc.sync.dma_start(kw[:, KEY_HEAD:POOL], k_rows[:, KEY_HEAD:POOL])
        nc.sync.dma_start(q_raw[:], qT[0].rearrange("(p j) w -> p j w", j=PACK))
        nc.scalar.dma_start(us_sb[:], us[0].rearrange("(p t) o -> p o t", t=PACK))
        v_head = keep.tile([P, V_HEAD], F32, name="v_head", align_bytes=256)
        nc.sync.dma_start(v_head[:], vT[0:P, 0:V_HEAD])
        make_identity(nc, ident[:], nomemset=True)

        kg = keep.tile([P, SLOTS], U32, name="kg", align_bytes=256)
        ksl = keep.tile([P, SLOTS], U8, name="ksl", align_bytes=256)
        ksg = keep.tile([P, SLOTS], U8, name="ksg", align_bytes=256)
        nc.vector.tensor_copy(
            ksl[:].rearrange("p (t s) -> p s t", t=PACK),
            ks[:].bitcast(U8).indirect(offsets[:]),
        )
        ksl_words = ksl[:].bitcast(I32)
        ksg_words = ksg[:].bitcast(I32)
        nc.vector.tensor_copy(ksg_words, ksl_words)
        for j in range(1, 4):
            nc.sync.dma_start(ksg_words[j:P:32, :], ksl_words[8 * j : P : 32, :])
        nc.vector.tensor_copy(
            kg[:].rearrange("p (t s) -> p s t", t=PACK),
            kw[:].bitcast(U32).indirect(offsets[:]),
        )
        v_raw = []
        for c in range(BLOCKS):
            v_raw.append(shared.tile([P, POOL], F32, name="v_raw%d" % c, align_bytes=256, offset=ROW * (c % 3)))
            first_column = V_HEAD if c == 0 else 0
            if c == BLOCKS - 1:
                first_column = LAST_HEAD
                nc.sync.dma_start(v_raw[c][:, 0:LAST_HEAD], vT[c * P : (c + 1) * P, 0:LAST_HEAD])
            nc.sync.dma_start(v_raw[c][:, first_column:POOL], vT[c * P : (c + 1) * P, first_column:POOL])

        wide = P * PACK
        q_pair = keep.tile([P, 2 * wide], BF16, name="q_pair", align_bytes=256)
        q_bf = [keep.tile([P, wide], BF16, name="q_bf%d" % b, align_bytes=256) for b in range(2)]
        q_bf += [q_pair[:, 0:wide], q_pair[:, wide : 2 * wide]]
        q_codes = keep.tile([P, NQ], U32, name="q_codes", align_bytes=256)
        q_scales = keep.tile([P, NQ], U8, name="q_scales", align_bytes=256)
        q_c = [q_codes[:, b * P : (b + 1) * P] for b in range(BLOCKS)]
        q_s = [q_scales[:, b * P : (b + 1) * P] for b in range(BLOCKS)]
        y_last = keep.tile([P, 2 * wide + SLOTS // 2], BF16, name="y_last", align_bytes=256)
        y_pair = [q_pair[:], y_last[:, 0 : 2 * wide]]
        y_bf = [y_pair[b // 2][:, (b % 2) * wide : (b % 2 + 1) * wide] for b in range(BLOCKS)]
        y_codes = keep.tile([P, NQ], U32, name="y_codes", align_bytes=256)
        y_scales = keep.tile([P, NQ], U8, name="y_scales", align_bytes=256)
        y_c = [y_codes[:, b * P : (b + 1) * P] for b in range(BLOCKS)]
        y_s = [y_scales[:, b * P : (b + 1) * P] for b in range(BLOCKS)]
        a_ps = [psum.tile([P, PACK, P], F32, name="a_ps%d" % b, offset=BANK * b) for b in range(BLOCKS)]

        def q_cast(b, copy):
            copy(
                q_bf[b][:].rearrange("p (c i t) -> p c t i", i=4, t=PACK),
                q_raw[:, :, b * P : (b + 1) * P].rearrange("p t (c i) -> p c t i", i=4),
            )

        def first(b):
            if b < 2:
                nc.vector.quantize_mx(out=q_c[b][:].bitcast(FP8X4), scales=q_s[b][:], in_=q_bf[b][:])
            if b == 2:
                half = slice(2 * P, NQ)
                nc.vector.quantize_mx(out=q_codes[:, half].bitcast(FP8X4), scales=q_scales[:, half], in_=q_pair[:])
            for t in range(PACK):
                cols = slice(t * P, (t + 1) * P)
                nc.tensor.matmul_mx(
                    out=a_ps[b][:, t, :],
                    lhsT=kg[:, cols].bitcast(FP8X4),
                    lhsT_scale=ksg[:, cols],
                    rhs=q_c[b][:].bitcast(FP8X4),
                    rhs_scale=q_s[b][:],
                    start=True,
                    stop=True,
                )

        def y_make(b):
            nc.vector.scalar_tensor_tensor(
                out=y_bf[b][:].rearrange("p (w t) -> p w t", t=PACK),
                in0=a_ps[b][:].rearrange("p t w -> p w t"),
                scalar=0.0,
                in1=us_sb[:].to_broadcast([P, P, PACK]),
                op0=ALU.max,
                op1=ALU.mult,
            )

        def y_quant(h):
            half = slice(2 * P * h, 2 * P * (h + 1))
            nc.vector.quantize_mx(out=y_codes[:, half].bitcast(FP8X4), scales=y_scales[:, half], in_=y_pair[h])

        for b in range(BLOCKS):
            q_cast(b, nc.vector.tensor_copy if b < 2 else nc.scalar.copy)
        nc.scalar.copy(v_raw[0][:, 0:V_HEAD], v_head[:])
        for b in range(BLOCKS):
            first(b)
        for b in range(3):
            y_make(b)
        y_quant(0)
        y_make(3)
        y_quant(1)

        def place(name, dtype, width, at):
            return shared.tile([P, width], dtype, name=name, align_bytes=256, offset=at)

        picked = [keep.tile([P, SLOTS], BF16, name="v_g0", align_bytes=256), y_last[:, 2 * wide - SLOTS // 2 : 2 * wide + SLOTS // 2]]
        picked += [place("v_g2", BF16, SLOTS, ROW), keep.tile([P, SLOTS], BF16, name="v_g3", align_bytes=256)]
        v_bf = [place("v_bf0", BF16, P * PACK, 3 * ROW + ROW // 2), place("v_bf1", BF16, P * PACK, 2 * ROW)]
        v_bf += [keep.tile([P, P * PACK], BF16, name="v_bf%d" % c, align_bytes=256) for c in range(2, BLOCKS)]
        turn_bank = [1, 2, 5, 6]

        def gather(c, vector_slots):
            cut = vector_slots // 16
            if cut == 0:
                nc.scalar.activation(picked[c][:], v_raw[c][:].indirect(offsets[:]), ACT.Copy)
            else:
                nc.vector.tensor_copy(picked[c][:, 0:vector_slots], v_raw[c][:].indirect(offsets[:, 0:cut]))
                nc.scalar.activation(
                    picked[c][:, vector_slots:SLOTS], v_raw[c][:].indirect(offsets[:, cut : SLOTS // 16]), ACT.Copy
                )
            words = picked[c][:].bitcast(F32)
            t_ps = psum.tile([P, 2, P], F32, name="t_ps%d" % c, offset=BANK * turn_bank[c])
            for u in range(2):
                nc.tensor.transpose(t_ps[:, u, :], words[:, u : 2 * P : 2], ident[:])
            return t_ps

        def turn(c, t_ps, pieces, copy):
            turned = v_bf[c][:].bitcast(F32).rearrange("p (e u) -> p e u", u=2)
            bank = t_ps[:].rearrange("p u e -> p e u")
            ne = P // pieces
            for h in range(pieces):
                copy(turned[:, ne * h : ne * (h + 1), :], bank[:, ne * h : ne * (h + 1), :])

        def quantise(values, codes, scales, pieces):
            ne = codes.shape[1] // pieces
            for h in range(pieces):
                nc.vector.quantize_mx(
                    out=codes[:, ne * h : ne * (h + 1)].bitcast(FP8X4),
                    scales=scales[:, ne * h : ne * (h + 1)],
                    in_=values[:, PACK * ne * h : PACK * ne * (h + 1)],
                )

        def second(codes, scales, banks):
            per_bank = BLOCKS // len(banks)
            width = codes.shape[1]
            sums = [psum.tile([P, per_bank, width], F32, name="o%d_%d" % (width, k), offset=BANK * k) for k in banks]
            for b in range(BLOCKS):
                nc.tensor.matmul_mx(
                    out=sums[b // per_bank][:, b % per_bank, :],
                    lhsT=y_c[b][:].bitcast(FP8X4),
                    lhsT_scale=y_s[b][:],
                    rhs=codes[:].bitcast(FP8X4),
                    rhs_scale=scales[:],
                    start=True,
                    stop=True,
                )
            return sums

        out_v = out[0].rearrange("(b p) e -> p b e", p=P)

        turn(0, gather(0, 0), 1, nc.scalar.copy)
        t_ps = gather(1, SLOTS // 2)
        codes01 = place("v_c01", U32, 2 * P, ROW + 2048)
        scales01 = keep.tile([P, 2 * P], U8, name="v_s01", align_bytes=256)
        quantise(v_bf[0], codes01[:, 0:P], scales01[:, 0:P], 1)
        early = psum.tile([P, 3, P], F32, name="early", offset=BANK * 7)
        for b in range(3):
            nc.tensor.matmul_mx(
                out=early[:, b, :],
                lhsT=y_c[b][:].bitcast(FP8X4),
                lhsT_scale=y_s[b][:],
                rhs=codes01[:, 0:P].bitcast(FP8X4),
                rhs_scale=scales01[:, 0:P],
                start=True,
                stop=True,
            )
        t_ps1 = t_ps
        t_ps = gather(2, SLOTS // 2)
        turn(1, t_ps1, 1, nc.scalar.copy)
        res_early = shared.tile([P, 3, P], F32, name="res_early", align_bytes=256, offset=2 * ROW + 2048)
        nc.scalar.copy(res_early[:], early[:])
        nc.sync.dma_start(out_v[:, 0:3, 0:P], res_early[:])
        quantise(v_bf[1], codes01[:, P : 2 * P], scales01[:, P : 2 * P], 1)
        o01 = second(codes01, scales01, [0, 1, 3, 4])
        turn(2, t_ps, 1, nc.scalar.copy)
        t_ps = gather(3, VECTOR_SLOTS)
        res1 = shared.tile([P, 3, P], F32, name="res1", align_bytes=256, offset=0)
        res01 = shared.tile([P, 1, 2 * P], F32, name="res01", align_bytes=256, offset=2048)
        codes2 = place("v_c2", U32, P, 4096)
        scales2 = keep.tile([P, P], U8, name="v_s2", align_bytes=256)
        quantise(v_bf[2], codes2, scales2, 1)
        nc.vector.tensor_copy(res01[:], o01[3][:])
        nc.sync.dma_start(out_v[:, 3:4, 0 : 2 * P], res01[:])
        for b in range(3):
            nc.scalar.copy(res1[:, b : b + 1, :], o01[b][:, :, P : 2 * P])
        nc.sync.dma_start(out_v[:, 0:3, P : 2 * P], res1[:])
        o2 = second(codes2, scales2, [2, 5])
        for h, queue in enumerate([nc.sync, nc.scalar]):
            res2 = keep.tile([P, 2, P], F32, name="res2_%d" % h, align_bytes=256)
            nc.scalar.copy(res2[:], o2[h][:])
            queue.dma_start(out_v[:, 2 * h : 2 * h + 2, 2 * P : 3 * P], res2[:])
        turn(3, t_ps, 2, nc.vector.tensor_copy)
        codes3 = keep.tile([P, P], U32, name="v_c3", align_bytes=256)
        scales3 = keep.tile([P, P], U8, name="v_s3", align_bytes=256)
        quantise(v_bf[3], codes3, scales3, 2)
        o3 = second(codes3, scales3, [7, 0, 1, 3])
        copies = [nc.vector.tensor_copy, nc.scalar.copy]
        queues = [nc.sync, nc.scalar]
        for b in range(BLOCKS):
            res3 = keep.tile([P, 1, P], F32, name="res3_%d" % b, align_bytes=256)
            copies[b % 2](res3[:], o3[b][:])
            queues[b % 2].dma_start(out_v[:, b : b + 1, 3 * P : 4 * P], res3[:])
